import numpy as np, ml_dtypes
CORES = [5,29,101,125,133,157,229,253]
N = 8
BF = ml_dtypes.bfloat16
def gentries(a):
    return np.ascontiguousarray(a.reshape(8, 16, -1).transpose(0, 2, 1)).reshape(8, -1)
def gtable(e):
    e = np.asarray(e); return np.ascontiguousarray(e.reshape(8, -1, 16).transpose(0, 2, 1)).reshape(128, -1).astype(np.int32)
W, K, O, TH, CAP, RO = 4096, 8, 256, 150, 48, 5
def ring(rng):
    gap = rng.integers(0, W // K, (N, 8, K, O)) + 1; gap[:, :, 0] = rng.integers(0, W, (N, 8, O))
    return np.add.accumulate(gap, axis=2) & (W - 1)
def held(c, want, pri):
    h = np.zeros(c.shape, np.int64)
    for q in range(N):
        for g in range(8):
            p = np.broadcast_to(pri[q, g], (K, O)); low = np.full(W, O); w = want[q, g]
            np.minimum.at(low, c[q, g][w], p[w]); h[q, g] = w & (low[c[q, g]] == p)
    return h
def crew(rng):
    c = ring(rng); lv = rng.choice(np.array([0, K // 2, K - 2, K - 1, K]), (8, O)); pri = np.zeros((8, O), np.int64); cls = np.zeros((8, 1, O), bool)
    nf = rng.permutation(8 + (O * 45 // 100 - 8) * np.arange(8) // 7)
    for g in range(8):
        n = int(nf[g]); o = rng.permutation(O); lv[g, o[:n]] = K; pri[g, o] = np.arange(O); cls[g, 0, o[:n]] = True
        for q in range(N):
            own = rng.permutation(W)[:n * K].reshape(K, n); c[q, g][:, o[:n]] = own
            rest = c[q, g][:, o[n:]]; t = rng.choice(own.reshape(-1), O - n); k = rng.integers(0, K, O - n)
            ok = (rng.random(O - n) < 0.3) & ~np.any(rest == t, axis=0)
            rest[k[ok], np.flatnonzero(ok)] = t[ok]; c[q, g][:, o[n:]] = rest
    want = (np.arange(K)[:, None] < lv[:, None, :]) & (cls | (rng.random((N, 8, K, O)) < 0.95))
    return c, held(c, want, np.broadcast_to(pri, (N, 8, O)))
def far(rng, m, share, over):
    k = rng.integers(0, K, (N, 8, O)); k = np.where(rng.random(k.shape) < 0.5, k, (K - 1) * rng.integers(0, 2, k.shape))
    hit = (rng.random((N, 8, 1, O)) < share) & (np.arange(K)[:, None] == k[:, :, None, :])
    return np.where(hit, TH + rng.integers(1, over + 1, m.shape), m)
def naps(rng, share):
    return np.add.reduce((rng.random((N, 8, O, RO)) < share).astype(np.int64) << np.arange(RO), axis=3)
def pack(x, c, h, m, wk, lump=None):
    ix = c.reshape(N, 8, 1, K * O); xc = np.take_along_axis(x, ix, 3); m = m.reshape(N, 8, 1, K * O)
    d = (m >> 4) + (((np.arange(16).reshape(16, 1) + ix) & 15) < (m & 15))
    if lump is not None:
        s = lump.reshape(N, 8, 1, K * O); i = (np.arange(16).reshape(16, 1) + s) & 15
        most = np.take_along_axis(np.maximum(xc, 255 - xc), i, 2).astype(np.int64); before = np.add.accumulate(most, axis=2) - most
        u = np.zeros(i.shape, np.int64); np.put_along_axis(u, i, np.minimum(np.maximum(m - before, 0), most), 2)
        d = np.where(s < 16, u, d)
    e = np.where(xc < 128, xc + d, xc - d)
    return {"x": np.ascontiguousarray(x.reshape(N, 128, W)).astype(np.float32).astype(BF), "snap": np.ascontiguousarray(e.reshape(N, 128, K * O)).astype(np.float32).astype(BF),
            "cs": np.stack([gtable(a.reshape(8, -1)) for a in c]), "hold": np.stack([gtable(a.reshape(8, -1)) for a in h]), "wake": np.stack([gtable(a) for a in wk])}
def cells(rng):
    return rng.integers(0, 256, (N, 8, 16, W), dtype=np.int32)
def setup_inputs(rng):
    x = cells(rng); c, h = crew(rng); m = far(rng, rng.integers(0, TH + 1, c.shape), 0.08, 600)
    return pack(x, c, h, m, naps(rng, rng.choice(np.array([0.5, 0.7, 0.9]), (N, 8, 1, 1))))
def setup_inputs_room(rng):
    x = cells(rng); c = np.zeros((N, 8, K, O), np.int64); h = np.ones((N, 8, K, O), np.int64); m = rng.integers(0, TH + 1, c.shape); wk = naps(rng, 0.7)
    cnt = rng.permutation(np.array([0, 1, CAP - 1, CAP, CAP + 1, 2 * CAP, O - 1, O]))
    for g in range(8):
        n = int(cnt[g]); o = rng.permutation(O)
        if n == 0: wk[:, g] = 1
        for q in range(N):
            c[q, g] = rng.permutation(W)[:K * O].reshape(K, O)
            rest = o[n:] if q & 1 else o[n:][rng.random(O - n) < 0.5]
            h[q, g][rng.integers(0, K, len(rest)), rest] = 0
            if q & 1 == 0 and n > 0: m[q, g][rng.integers(0, K), rest[rng.random(len(rest)) < 0.15]] = TH + 1
    return pack(x, c, h, m, wk)
def setup_inputs_storm(rng):
    x = cells(rng); c = ring(rng); m = rng.integers(0, TH + 1, c.shape); want = rng.random(c.shape) < 0.5; wk = naps(rng, 0.8)
    pri = np.argsort(rng.random((N, 8, O)), axis=-1); deal = rng.permutation(8); role = deal & 3
    for g in range(8):
        if deal[g] == 0:
            want[:, g] = True
            for q in range(N): c[q, g] = rng.permutation(W)[:K * O].reshape(K, O)
        if role[g] == 0: m[:, g, rng.integers(0, K)] = TH + 1 + rng.integers(0, 600, (N, O))
        if role[g] == 1: m[::2, g, 0, ::2] = TH + 1
        if role[g] == 2:
            o = int(rng.integers(0, O))
            for q in range(N):
                v = int(rng.integers(0, W)); k = rng.integers(0, K, O); ok = ~np.any(c[q, g] == v, axis=0)
                c[q, g][k[ok], np.flatnonzero(ok)] = v; x[q, g, :, v] = rng.integers(0, 16, 16) + 240 * (q & 1)
                want[q, g, :, o] = True; i = int(np.flatnonzero(pri[q, g] == 0)[0]); pri[q, g, i] = pri[q, g, o]; pri[q, g, o] = 0
        if role[g] == 3: want[:, g] = False; wk[:, g] = wk[:, g] & ~1
    p = 2 * int(rng.integers(0, N // 2)); m[p:p + 2] = far(rng, m, 1.0, 600)[p:p + 2]
    return pack(x, c, held(c, want, pri), m, wk)
def setup_inputs_crowd(rng):
    x = cells(rng); c = np.zeros((N, 8, K, O), np.int64)
    for q in range(N):
        for g in range(8):
            P = 64 if g & 1 else 256
            pool = rng.permutation(np.concatenate([np.array([0, W - 1]), 1 + rng.permutation(W - 2)[:P - 2]]))
            c[q, g] = pool[(rng.integers(0, P, O) + np.arange(K)[:, None] * (2 * rng.integers(0, P // 2, O) + 1)) & (P - 1)]
    pri = np.argsort(rng.random((8, O)), axis=-1); lv = np.where(pri < 3, K, rng.integers(0, K + 1, (8, O)))
    lv[rng.permutation(8)[:4]] = 0
    want = np.broadcast_to(np.arange(K)[:, None] < lv[:, None, :], (N, 8, K, O))
    m = far(rng, rng.integers(0, TH + 1, c.shape), 0.01, 600)
    return pack(x, c, held(c, want, np.broadcast_to(pri, (N, 8, O))), m, naps(rng, rng.choice(np.array([0.6, 1.0]), (N, 8, 1, 1))))
def setup_inputs_ties(rng):
    x = cells(rng); z = rng.random((N, 8, 1, W)); x = np.where(z < 0.06, 0, np.where(z < 0.12, 255, x)).astype(np.int32)
    c, h = crew(rng); m = far(rng, rng.choice(np.array([0, TH - 1, TH]), c.shape), 0.12, 1)
    wk = naps(rng, 0.75) & ~(1 << int(rng.integers(1, 3)))
    return pack(x, c, h, m, wk, np.minimum(rng.integers(0, 32, c.shape), 16))
def setup_inputs_spread(rng):
    x = np.minimum((np.exp2(8.01 * rng.random((N, 8, 1, W))) * rng.random((N, 8, 16, W))).astype(np.int32), 255)
    c, h = crew(rng); m = far(rng, (TH * rng.random(c.shape) ** 4).astype(np.int64), 0.1, 1000)
    share = np.ones((N, 1, 1, 1)) * rng.permutation(np.array([0.0, 0.2, 0.4, 0.6, 0.8, 0.9, 1.0, 1.0])).reshape(1, 8, 1, 1)
    return pack(x, c, h, m, naps(rng, share))
def check_inputs(d):
    bad = []
    for k in ("x", "snap"):
        v = np.asarray(d[k]).astype(np.float32)
        if not (np.all(v >= 0) and np.all(v <= 255) and np.all(v == np.floor(v))): bad.append("range of " + k)
    for k, hi in (("cs", W - 1), ("hold", 1), ("wake", 2 ** RO - 1)):
        if np.min(d[k]) < 0 or np.max(d[k]) > hi: bad.append("range of " + k)
    c = np.stack([gentries(a) for a in d["cs"]]).reshape(N, 8, K, O); h = np.stack([gentries(a) for a in d["hold"]]).reshape(N, 8, K, O)
    s = np.sort(c, axis=2)
    if np.any(s[:, :, 1:] == s[:, :, :-1]): bad.append("cells of an operation differ")
    for q in range(N):
        for g in range(8):
            v = c[q, g][h[q, g] == 1]
            if len(np.unique(v)) != len(v) and "a cell has one holder" not in bad: bad.append("a cell has one holder")
    return bad
def reference(x, snap, cs, hold, wake):
    v = np.zeros((N, 8, 16, W + 1), np.int32)
    v[..., :W] = x.astype(np.float32).astype(np.int32).reshape(N, 8, 16, W)
    e = snap.astype(np.float32).astype(np.int32).reshape(N, 8, 16, K * O)
    c = np.stack([gentries(a) for a in cs]).astype(np.int64).reshape(N, 8, K, O); h = np.stack([gentries(a) for a in hold]).reshape(N, 8, K, O)
    wk = np.stack([gentries(a) for a in wake]).astype(np.int64)
    own = np.arange(O) + 1; lane = np.broadcast_to(np.arange(O), (N, 8, O)); cur = np.array(lane)
    lock = np.zeros((N, 8, W + 1), np.int64)
    np.put_along_axis(lock, np.where(h == 1, c, W).reshape(N, 8, -1), np.broadcast_to(own, c.shape).reshape(N, 8, -1), 2)
    for t in range(RO):
        twin = np.arange(N) ^ (1 + t % (N - 1))
        got = np.take_along_axis(v, c.reshape(N, 8, 1, -1), 3)
        dist = np.add.reduce(np.abs(got - e), axis=2).reshape(N, 8, K, O)
        who = np.take_along_axis(lock, c.reshape(N, 8, -1), 2).reshape(N, 8, K, O); mine = who == own
        bad = np.any(dist > TH, axis=2); full = np.all(mine, axis=2)
        abort = bad | bad[twin]; ready = full & full[twin] & ~abort
        before = np.add.accumulate(ready.astype(np.int64), axis=2) - ready
        commit = ready & (before < CAP); done = abort | commit
        first = np.argmin(mine, axis=2)[:, :, None, :]
        cell = np.take_along_axis(np.take_along_axis(c, first, 2)[:, :, 0], cur, 2); by = np.take_along_axis(np.take_along_axis(who, first, 2)[:, :, 0], cur, 2)
        gone = np.take_along_axis(done, cur, 2); act = (((wk >> t) & 1) == 1) & ~gone & ~np.take_along_axis(full, cur, 2)
        np.put_along_axis(lock, np.where(done[:, :, None, :] & mine, c, W).reshape(N, 8, -1), 0, 2)
        for q in range(N):
            for g in range(8):
                w = np.flatnonzero(act[q, g] & (by[q, g] == 0)); low = np.full(W, O); a = cell[q, g][w]
                np.minimum.at(low, a, w); win = low[a] == w
                lock[q, g][a[win]] = cur[q, g][w[win]] + 1
        cur = np.where(gone, lane, np.where(act & (by > 0), by - 1, cur))
        cm = np.broadcast_to(commit[:, :, None, :], (N, 8, K, O)); dn = np.broadcast_to(done[:, :, None, :], (N, 8, K, O)).reshape(N, 8, 1, -1)
        d = np.where(cm.reshape(N, 8, 1, -1), got[twin], e)
        np.put_along_axis(v, np.where(cm, c, W).reshape(N, 8, 1, -1), d, 3)
        u = np.add.reduce(d.reshape(N, 8, 2, 8, K, O).astype(np.int64), axis=3); hs = (u[:, :, 0] * u[:, :, 1]) >> 3
        new = np.zeros((N, 8, K, O), np.int64); new[:, :, 0] = hs[:, :, 0] & (W - 1)
        for k in range(1, K): new[:, :, k] = (new[:, :, k - 1] + 1 + (hs[:, :, k] & (W // K - 1))) & (W - 1)
        c = np.where(done[:, :, None, :], new, c)
        e = np.where(dn, np.take_along_axis(v, c.reshape(N, 8, 1, -1), 3), e)
    lock[..., W] = 0
    mine = np.take_along_axis(lock, c.reshape(N, 8, -1), 2).reshape(N, 8, K, O) == own
    ys = np.add.reduce(v[..., :W] * np.arange(1, 17, dtype=np.int32).reshape(16, 1), axis=2)
    return {"ys": ys.astype(np.float32), "yc": np.stack([gtable(a.reshape(8, -1)) for a in c]).astype(np.float32),
            "yh": np.stack([gtable(a.reshape(8, -1)) for a in mine]).astype(np.float32), "yl": np.stack([gtable(a) for a in cur]).astype(np.float32)}

@@ -1,0 +1,648 @@
+import math
+from concourse.mybir import AluOpType as OP, ActivationFunctionType as AF
+
+STEPS = 5
+E0, VB, DB, E1, VE = 0, 2048, 6144, 6528, 8576
+LW = 4112
+
+SCRATCH = {
+    "V": ("sbuf", [128, VE], "bfloat16"),
+    "got0": ("sbuf", [128, 2048], "bfloat16"), "got1": ("sbuf", [128, 2048], "bfloat16"),
+    "mx": ("sbuf", [128, 2048], "bfloat16"), "cR": ("sbuf", [128, 2048], "float32"),
+    "IW": ("sbuf", [128, LW], "float32"), "LK": ("sbuf", [128, 6144], "float32"),
+    "LV0": ("sbuf", [128, 2048], "float32"), "LV": ("sbuf", [128, 256], "float32"),
+    "SEL2": ("sbuf", [128, 2048], "bfloat16"), "SELPK": ("sbuf", [128, 2048], "bfloat16"), "SELW": ("sbuf", [128, 2048], "bfloat16"),
+    "MK": ("sbuf", [128, 256], "bfloat16"), "PKP": ("sbuf", [128, 128], "bfloat16"), "PKO": ("sbuf", [128, 128], "bfloat16"),
+    "PKH": ("sbuf", [128, 128], "float16"), "PK8": ("sbuf", [128, 128], "bfloat16"),
+    "B8": ("sbuf", [128, 8], "bfloat16"), "B8H": ("sbuf", [128, 8], "float16"),
+    "q0": ("sbuf", [128, 256], "bfloat16"), "q1": ("sbuf", [128, 256], "bfloat16"), "qh": ("sbuf", [128, 256], "float16"),
+    "EQ": ("sbuf", [128, 4096], "bfloat16"), "LH": ("sbuf", [128, 128], "bfloat16"),
+    "ONE": ("sbuf", [128, 256], "bfloat16"), "ZB": ("sbuf", [128, 256], "bfloat16"), "OPW": ("sbuf", [128, 512], "bfloat16"),
+    "B128": ("sbuf", [128, 128], "bfloat16"), "BTM": ("sbuf", [128, 128], "bfloat16"), "ID": ("sbuf", [128, 128], "bfloat16"),
+    "OR": ("sbuf", [128, 256], "float32"), "JC": ("sbuf", [128, 256], "float32"), "K": ("sbuf", [128, 256], "float32"),
+    "COMP": ("sbuf", [128, 512], "float32"), "DUM": ("sbuf", [128, 48], "float32"), "thrR": ("sbuf", [128, 256], "float32"),
+    "clOp": ("sbuf", [128, 256], "float32"), "clR": ("sbuf", [128, 256], "float16"),
+    "G1": ("sbuf", [128, 256], "bfloat16"), "decR": ("sbuf", [128, 256], "bfloat16"), "decL": ("sbuf", [128, 256], "bfloat16"),
+    "dnR": ("sbuf", [128, 256], "bfloat16"), "gnR": ("sbuf", [128, 256], "bfloat16"), "winR": ("sbuf", [128, 256], "bfloat16"),
+    "Dl": ("sbuf", [128, 384], "bfloat16"), "yso": ("sbuf", [128, 256], "float32"),
+    "i1": ("sbuf", [128, 8], "int32"), "col": ("sbuf", [128, 32], "float32"), "GC": ("sbuf", [128, 8], "float32"),
+    "lane": ("sbuf", [128, 656], "float32"), "red": ("sbuf", [128, 128], "float32"),
+    "code0": ("sbuf", [128, 16], "float32"), "code1": ("sbuf", [128, 16], "float32"),
+    "rdy": ("sbuf", [128, 16], "bfloat16"), "rw": ("sbuf", [128, 16], "bfloat16"), "cab": ("sbuf", [128, 32], "bfloat16"),
+    "Ls": ("sbuf", [128, 72], "int32"), "Lt": ("sbuf", [128, 48], "float32"), "L16": ("sbuf", [128, 48], "uint16"),
+}
+for _n in ("csI", "hdI", "kI", "Pi", "A", "Bv", "pr", "h", "yI0", "yI1"):
+    SCRATCH[_n] = ("sbuf", [128, 128], "int32")
+for _n in ("HB", "kp1", "NCE", "sm", "d1", "bd", "cmS", "key", "jW", "eaA", "ejA", "eaB", "ejB", "t1", "t2", "t3", "t4", "t5"):
+    SCRATCH[_n] = ("sbuf", [128, 128], "float32")
+for _n in ("c16", "ei16"):
+    SCRATCH[_n] = ("sbuf", [128, 128], "uint16")
+for _n in ("wkI", "keI", "ceI", "fkI", "acI"):
+    SCRATCH[_n] = ("sbuf", [128, 16], "int32")
+for _n in ("cl16", "cur16", "lc16", "p16", "dn16", "off16", "oo16", "ol16", "dec16"):
+    SCRATCH[_n] = ("sbuf", [128, 16], "uint16")
+for _t in range(STEPS):
+    SCRATCH["lb%d" % _t] = ("sbuf", [128, 2048], "bfloat16")
+    SCRATCH["lc%d" % _t] = ("sbuf", [128, 16], "float32")
+    SCRATCH["ln%d" % _t] = ("sbuf", [128, 128], "int32")
+for _n in ("PSP", "PSM", "PSC", "PSR", "PSA", "PSD", "V0", "V1"):
+    SCRATCH[_n] = ("psum", [128, 512], "float32")
+
+MSG = ("b0", "b1", "co", "nc")
+SEMAPHORES = ["qv", "qs", "qt", "qg"] + ["d%d" % i for i in range(28)]
+for _t in range(STEPS):
+    for _m in MSG:
+        SEMAPHORES += ["a%s%d" % (_m, _t), "l%s%d" % (_m, _t)]
+
+_L = {}
+for _i, _n in enumerate("cur cl clS p act nf an mv cand ac aw wW dm256 dm4096 win cur1 x1 x2 x3 x4 x5 x6 X rank inc e cm done n32 n32a wo "
+                        "keyv full tr z lm fk1 dec val".split()):
+    _L[_n] = 16 * _i
+
+
+def landing(m, t):
+    if m == "b0": return "lb%d" % t, 0, 1024
+    if m == "b1": return "lb%d" % t, 1024, 2048
+    if m == "co": return "lc%d" % t, 0, 16
+    return "ln%d" % t, 0, 128
+
+
+def route(core, t, T, topo):
+    dst = T.cores[T.rank_of(core) ^ (1 + t % 7)]
+    near = [x for x in topo.cores_of(core) if x != core and topo.die(x) == topo.die(core) and topo.may_write(x, dst)]
+    far = [x for x in topo.cores_of(core) if topo.die(x) != topo.die(core) and topo.may_write(x, dst)]
+    via = {"b0": near[-1], "b1": near[-2], "co": None, "nc": None}
+    if not topo.may_write(core, dst):
+        via["co"] = far[0]; via["nc"] = far[1]
+    return dst, via
+
+
+def engines8(topo, a, b):
+    return sum(1 << e for e in topo.engines(a, b)[:8])
+
+
+def send(g, T, topo, core, dst, m, t, src):
+    buf, lo, hi = landing(m, t)
+    rid, pid = topo.addr(dst, core)
+    return g.remote_dma(out_ap=T[buf][:, lo:hi], in_ap=src, remote_sem=T.sem["a%s%d" % (m, t)], local_sem=T.sem["l%s%d" % (m, t)],
+                        pid=pid, routing_id=rid, dma_engine_mask=engines8(topo, core, dst))
+
+
+def relay_program(g, core, T, topo):
+    for src in [x for x in topo.cores_of(core) if T.rank_of(x) is not None]:
+        for t in range(STEPS):
+            dst, via = route(src, t, T, topo)
+            mine = [m for m in MSG if via[m] == core]
+            for m in mine:
+                buf, lo, hi = landing(m, t)
+                g.wait_ge(T.sem["a%s%d" % (m, t)], 8)
+                send(g, T, topo, core, dst, m, t, T[buf][:, lo:hi])
+            for m in mine:
+                g.wait_ge(T.sem["l%s%d" % (m, t)], 8)
+
+
+def rank_program(g, core, T, topo):
+    if T.rank_of(core) is None:
+        relay_program(g, core, T, topo)
+        return
+    Q = {"v": g.vector, "s": g.scalar, "t": g.tensor, "y": g.sync, "g": g}
+    width = {n: b[1][1] for n, b in SCRATCH.items()}
+    ispsum = {n: b[0] == "psum" for n, b in SCRATCH.items()}
+    hist = {}
+    ops = []
+    known = {q: {} for q in Q}
+    cnt = {}
+    nd = [0]
+
+    def R(b, lo=0, hi=None, st=1, np=128):
+        return ("n", b, lo, width[b] if hi is None else hi, st, np)
+
+    def L(n, a=0, b=16):
+        return ("n", "lane", _L[n] + a, _L[n] + b, 1, 128)
+
+    def C(i):
+        return ("n", "col", i, i + 1, 1, 128)
+
+    def IX(w, o):
+        return ("i", w, o)
+
+    def ap(s):
+        if s[0] == "i": return ap(s[1]).indirect(ap(s[2]))
+        p = slice(0, s[5]) if s[5] < 128 else slice(None)
+        if s[4] == 1: return T[s[1]][p, s[2]:s[3]]
+        return T[s[1]][p, s[2]:s[3]:s[4]]
+
+    def flat(s):
+        if not isinstance(s, tuple): return []
+        if s[0] == "i": return flat(s[1]) + flat(s[2])
+        return [(s[1], s[2], s[3])]
+
+    def need(q, deps):
+        for d in sorted(deps, reverse=True):
+            _, sem, n, kn = ops[d]
+            if known[q].get(sem, 0) >= n: continue
+            Q[q].wait_ge(T.sem[sem], n)
+            for k2, v2 in kn.items():
+                if known[q].get(k2, 0) < v2: known[q][k2] = v2
+
+    def track(q, reads, writes, kind):
+        deps = set()
+        acc = [(b, lo, hi, False) for b, lo, hi in reads] + [(b, lo, hi, True) for b, lo, hi in writes]
+        for b, lo, hi, w in acc:
+            for lo2, hi2, w2, d in hist.get(b, ()):
+                meet = lo < hi2 and lo2 < hi and (w or w2)
+                if ispsum.get(b, False):
+                    if ops[d][0] != q or (q != "t" and meet): deps.add(d)
+                elif meet:
+                    deps.add(d)
+        return deps, acc
+
+    def record(q, acc, sem, n):
+        kn = dict(known[q]) if q in known else {}
+        kn[sem] = n
+        ops.append((q, sem, n, kn))
+        d = len(ops) - 1
+        for b, lo, hi, w in acc:
+            hl = hist.setdefault(b, [])
+            if w and not ispsum.get(b, False):
+                hist[b] = hl = [x for x in hl if not (lo <= x[0] and x[1] <= hi)]
+            elif ispsum.get(b, False):
+                hist[b] = hl = [x for x in hl if not (ops[x[3]][0] == q and lo <= x[0] and x[1] <= hi and (w or not x[2]))]
+            hl.append((lo, hi, w, d))
+
+    def comp(q, reads, writes, fn):
+        deps, acc = track(q, sum((flat(r) for r in reads), []), sum((flat(w) for w in writes), []), "c")
+        for w in writes:
+            if w[0] == "i":
+                acc = [(b, lo, hi, (wr and b != w[2][1])) for b, lo, hi, wr in acc]
+        need(q, deps)
+        sem = "q" + q
+        cnt[sem] = cnt.get(sem, 0) + 1
+        fn().then_inc(T.sem[sem], 1)
+        record(q, acc, sem, cnt[sem])
+
+    def dma(q, out, in_, reads, writes):
+        deps, acc = track(q, reads, writes, "d")
+        need(q, deps)
+        sem = "d%d" % nd[0]; nd[0] += 1
+        Q[q].dma_start(out, in_).then_inc(T.sem[sem], 16)
+        cnt[sem] = 16
+        record(q, acc, sem, 16)
+
+    def tt(out, a, b, op):
+        comp("v", [a, b], [out], lambda: g.vector.tensor_tensor(out=ap(out), in0=ap(a), in1=ap(b), op=op))
+
+    def ts(out, a, s1, op0, s2=None, op1=None):
+        x1 = ap(s1) if isinstance(s1, tuple) else s1
+        x2 = ap(s2) if isinstance(s2, tuple) else s2
+        if op1 is None:
+            comp("v", [a, s1], [out], lambda: g.vector.tensor_scalar(out=ap(out), in0=ap(a), scalar1=x1, scalar2=None, op0=op0))
+        else:
+            comp("v", [a, s1, s2], [out], lambda: g.vector.tensor_scalar(out=ap(out), in0=ap(a), scalar1=x1, scalar2=x2, op0=op0, op1=op1))
+
+    def cp(out, a):
+        comp("v", [a], [out], lambda: g.vector.tensor_copy(out=ap(out), in_=ap(a)))
+
+    def fill(out, x):
+        comp("v", [], [out], lambda: g.vector.memset(ap(out), x))
+
+    def act(out, a, func=AF.Copy, scale=1.0, bias=None):
+        sc = ap(scale) if isinstance(scale, tuple) else scale
+        if bias is None:
+            comp("s", [a, scale], [out], lambda: g.scalar.activation(out=ap(out), in_=ap(a), func=func, scale=sc))
+        else:
+            comp("s", [a, scale, bias], [out], lambda: g.scalar.activation(out=ap(out), in_=ap(a), func=AF.Identity, bias=ap(bias), scale=sc))
+
+    def scatter_act(out, a):
+        comp("s", [a], [out], lambda: g.scalar.activation(out=ap(out), in_=ap(a), func=AF.Silu))
+
+    def mm(out, lhsT, rhs, start, stop):
+        comp("t", [lhsT, rhs], [out], lambda: g.tensor.matmul(ap(out), ap(lhsT), ap(rhs), start, stop))
+
+    def iota(out, pattern, base, cm):
+        comp("g", [], [out], lambda: g.iota(ap(out), pattern, base, cm, allow_small_or_imprecise_dtypes=True))
+
+    def asel(out, a, pattern, op, base, cm):
+        comp("g", [a], [out], lambda: g.affine_select(ap(out), ap(a), pattern, op, 0.0, base, cm))
+
+    def conv1(bank, parts):
+        for h in range(2):
+            for n, (src, np, pick) in enumerate(parts):
+                mm(R(bank, 256 + 128 * h, 384 + 128 * h), R(src, 128 * h, 128 * h + 128, 1, np), pick, n == 0, n == len(parts) - 1)
+
+    def conv2(bank, lo, q, b8="B8"):
+        tt(R(q), R(bank, 256, 512), R("MK"), OP.mult)
+        for h in range(2):
+            mm(R(bank, lo + 8 * h, lo + 8 * h + 8), R(q, 128 * h, 128 * h + 128), R(b8), True, True)
+
+    def out_send(t, m, srcspec):
+        dst, via = route(core, t, T, topo)
+        to = dst if via[m] is None else via[m]
+        deps, acc = track("g", flat(srcspec), [], "r")
+        need("g", deps)
+        send(g, T, topo, core, to, m, t, ap(srcspec))
+        sem = "l%s%d" % (m, t)
+        cnt[sem] = 8
+        record("g", acc, sem, 8)
+
+    def arrive(t, m):
+        buf, lo, hi = landing(m, t)
+        sem = "a%s%d" % (m, t)
+        cnt[sem] = 8
+        record("net", [(buf, lo, hi, True)], sem, 8)
+
+    BIG = 1.0e6
+    for t in range(STEPS):
+        for m in MSG: arrive(t, m)
+    Pc, PsE, Pdp, Pt = (R("V0", 128 * i, 128 * i + 128) for i in range(4))
+    Pthr, Pk, Pkb, Pu = (R("V1", 128 * i, 128 * i + 128) for i in range(4))
+
+    dma("y", T.csI[:], T.cs[:], [], [("csI", 0, 128)])
+    dma("y", T.hdI[:], T.hold[:], [], [("hdI", 0, 128)])
+    dma("y", T.V[:, VB:DB], T.x[:], [], [("V", VB, DB)])
+    dma("y", T.V[:, E0:E0 + 2048], T.snap[:], [], [("V", E0, E0 + 2048)])
+    dma("y", T.wkI[:], T.wake[:], [], [("wkI", 0, 16)])
+    fill(R("ONE"), 1.0)
+    iota(R("i1", 0, 1), [[0, 1]], 0, 1)
+    asel(R("BTM"), R("ONE", 0, 128), [[-16, 8], [0, 16]], OP.is_ge, 0, 1)
+    asel(R("B128"), R("BTM"), [[16, 8], [0, 16]], OP.is_ge, 15, -1)
+    iota(R("kI"), [[1, 8], [0, 16]], 0, 0)
+    iota(R("eaA"), [[16, 128]], 0, 0)
+    asel(R("q1", 0, 128), R("B128"), [[-1, 128]], OP.is_ge, 0, 1)
+    asel(R("ID"), R("B128"), [[-1, 128]], OP.is_equal, 0, 1)
+    iota(R("OR"), [[1, 256]], 0, 0)
+    iota(R("clOp"), [[0, 16], [1, 16]], 0, 0)
+    iota(R("IW"), [[1, LW]], 0, 0)
+    fill(R("SEL2"), 0.0)
+    for i in range(16):
+        ts(R("SEL2", 129 * i, 128 * i + 128, 16), R("B128", i, 128, 16), 2.0, OP.mult)
+    ts(R("i1", 1, 2), R("i1", 0, 1), 15, OP.bitwise_and)
+    ts(R("i1", 2, 3), R("i1", 0, 1), 1, OP.bitwise_and)
+    ts(R("i1", 3, 4), R("i1", 1, 2), 1, OP.arith_shift_right)
+    cp(C(0), R("i1", 1, 2))
+    cp(C(1), R("i1", 2, 3))
+    ts(C(2), C(1), -1.0, OP.mult, 1.0, OP.add)
+    ts(C(3), R("i1", 3, 4), 256.0, OP.mult)
+    ts(C(4), C(0), 8.0, OP.is_lt, 0.5 - 1024.0, OP.mult)
+    ts(C(5), C(4), 1024.0, OP.add)
+    ts(C(9), C(1), 64.0, OP.add)
+    ts(R("SELPK"), R("SEL2"), C(5), OP.mult)
+    cp(Pk, R("kI"))
+    ts(R("jW"), R("eaA"), C(0), OP.add)
+    ts(R("t5"), R("jW"), 4096.0, OP.add)
+    cp(Pc, R("csI"))
+    cp(R("c16"), Pc)
+    ts(R("LV0", 0, 256), R("OR"), C(2), OP.mult, C(9), OP.add)
+    cp(R("t1"), R("hdI"))
+    tt(R("t3"), Pc, R("t5"), OP.subtract)
+    tt(R("t3"), R("t3"), R("t1"), OP.mult)
+    tt(R("t3"), R("t3"), R("t5"), OP.add)
+    cp(R("ei16"), R("t3"))
+    cp(R("LV0", 256, 512), R("LV0", 0, 256))
+    cp(R("LV0", 512, 1024), R("LV0", 0, 512))
+    cp(R("LV0", 1024, 2048), R("LV0", 0, 1024))
+    fill(R("LK", 0, LW), 0.0)
+
+    Ecur = [E0]
+
+    def P_chunk(buf, lo, h):
+        for i in range(16):
+            mm(R("PSP", 64 * h, 64 * h + 64), R("SELPK", 128 * i, 128 * i + 128), R(buf, lo + 1024 * h + i, lo + 1024 * h + 1024, 16), i == 0, i == 15)
+
+    def hash_front():
+        cp(R("Pi"), R("PSP", 0, 128))
+        ts(R("A"), R("Pi"), 2047, OP.bitwise_and)
+        ts(R("Bv"), R("Pi"), 11, OP.arith_shift_right)
+        tt(R("sm"), R("A"), R("Bv"), OP.add)
+
+    def hash_back(y):
+        tt(R("pr"), R("A"), R("Bv"), OP.mult)
+        ts(R("h", 0, 16), R("pr", 0, 16), 3, OP.arith_shift_right, 4095, OP.bitwise_and)
+        ts(R("h", 16, 128), R("pr", 16, 128), 3, OP.arith_shift_right, 511, OP.bitwise_and)
+        for k in range(1, 8):
+            tt(R("h", 16 * k, 16 * k + 16), R("h", 16 * k, 16 * k + 16), R("h", 16 * k - 16, 16 * k), OP.add)
+        tt(R(y), R("h"), Pk, OP.add)
+        ts(R(y), R(y), 4095, OP.bitwise_and)
+
+    def lanes_win():
+        tt(R("winR", 0, 256, 1, 8), R("PSA", 0, 256, 1, 8), R("thrR", 0, 256, 1, 8), OP.is_le)
+        conv1("PSD", [("winR", 8, R("PK8", 0, 128, 1, 8))])
+
+    def gather_front(t, between):
+        gt = "got%d" % (t & 1)
+        for h in range(2):
+            lo = 1024 * h
+            if h == 1 and t > 0: lanes_win()
+            act(R(gt, lo, lo + 1024), IX(R("V", VB, DB), R("c16", 64 * h, 64 * h + 64)))
+            tt(R("mx", lo, lo + 1024), IX(R("V", VB, DB), R("c16", 64 * h, 64 * h + 64)), R("V", Ecur[0] + lo, Ecur[0] + lo + 1024), OP.max)
+            out_send(t, "b%d" % h, R(gt, lo, lo + 1024))
+            if h == 0: P_chunk(gt, 0, h)
+        for h in range(2):
+            if h == 1:
+                if t > 0: conv2("PSD", 0, "q1")
+                P_chunk(gt, 0, h)
+                between()
+            for i in range(16):
+                mm(R("PSM", 64 * h, 64 * h + 64), R("SEL2", 128 * i, 128 * i + 128), R("mx", 1024 * h + i, 1024 * h + 1024, 16), i == 0, i == 15)
+
+    def list_table():
+        act(R("cR"), IX(R("IW", 0, 4096), R("c16")), scale=2048.0)
+        dma("y", T.K[0:128:2, :], T.cR[0:128:16, :], [("cR", 0, 2048)], [("K", 0, 256)])
+        dma("y", T.K[1:128:2, :], T.cR[0:128:16, :], [("cR", 0, 2048)], [("K", 256, 512)])
+
+    def tree(src, out, op):
+        tt(R("red", 0, 64), R(src, 0, 64), R(src, 64, 128), op)
+        tt(R("red", 64, 96), R("red", 0, 32), R("red", 32, 64), op)
+        tt(out, R("red", 64, 80), R("red", 80, 96), op)
+
+    def flags_front():
+        hash_front()
+        tt(R("d1"), R("PSM", 0, 128), R("sm"), OP.subtract)
+        tt(R("bd"), R("d1"), Pthr, OP.is_gt)
+        tree("bd", L("tr"), OP.add)
+
+    for h in range(2): P_chunk("V", E0, h)
+    hash_front()
+    cp(PsE, R("sm"))
+    gather_front(0, lambda: None)
+    hash_back("yI1")
+    cp(R("NCE"), R("yI1"))
+    ts(Pthr, PsE, 150.0, OP.add)
+    ts(R("t2"), R("t1"), -1.0 / 32, OP.mult, 1.0 / 32, OP.add)
+    tree("t2", L("n32"), OP.add)
+    flags_front()
+    tt(R("code0"), L("tr"), L("n32"), OP.add)
+    out_send(0, "co", R("code0"))
+    hash_back("yI0")
+    out_send(0, "nc", R("yI0"))
+    cp(L("cur"), R("jW", 0, 16)); cp(R("cur16"), L("cur"))
+    scatter_act(IX(R("LK"), R("ei16")), R("LV0"))
+    list_table()
+    lna = math.log(1.75)
+    ts(L("lm"), R("jW", 0, 16), -128.0, OP.add)
+    act(L("wW"), L("lm"), AF.Exp, -lna)
+    ts(R("thrR"), R("OR"), -128.0, OP.add)
+    act(R("thrR"), R("thrR"), AF.Exp, -lna)
+    ts(R("thrR"), R("thrR"), 2.5, OP.mult)
+    ts(Pkb, Pk, 4096.0, OP.mult)
+    ts(R("t1"), R("t1"), 65536.0, OP.mult)
+    tt(R("HB"), R("t1"), Pkb, OP.add)
+    ts(R("kp1"), Pk, 1.0, OP.add)
+    ts(C(6), C(0), 0.0, OP.is_equal)
+    ts(C(7), C(0), 1.0, OP.is_equal)
+    ts(C(8), C(0), 1.0, OP.add, 0.5, OP.mult)
+    for t in range(STEPS):
+        ts(C(10 + t), C(1), float(t + 2), OP.mult, 64.0, OP.add)
+    fill(C(16), -2048.0); fill(C(17), -64.0)
+    ts(R("PKP"), R("B128"), C(6), OP.mult)
+    ts(R("PKH"), R("B128"), C(6), OP.mult)
+    ts(R("PKO"), R("B128"), C(7), OP.mult)
+    cp(R("B8"), R("B128", 0, 128, 16))
+    cp(R("B8H"), R("B128", 0, 128, 16))
+    ts(R("MK"), R("clOp"), C(0), OP.is_equal)
+    mm(R("PSD", 0, 128, 1, 8), R("PKP", 0, 128, 16), R("PKP"), True, True)
+    cp(R("PK8", 0, 128, 1, 8), R("PSD", 0, 128, 1, 8))
+    ts(R("JC"), R("OR"), C(3), OP.add)
+    ts(R("DUM", 0, 24), R("jW", 0, 24), 4096.0, OP.add, 2048.0, OP.mult)
+    ts(R("DUM", 24, 48), R("jW", 0, 24), 4096.0, OP.add, 2048.0, OP.mult)
+    ts(L("dm256"), R("jW", 0, 16), 256.0, OP.add)
+    ts(L("dm4096"), R("jW", 0, 16), 4096.0, OP.add)
+    fill(L("z"), 0.0); fill(L("dec"), 0.0); fill(R("ZB"), 0.0)
+    fill(R("V", DB, E1), 0.0)
+    ts(R("BTM"), R("q1", 0, 128), -1.0, OP.mult)
+    cp(R("dec16"), L("dec"))
+
+    def renew_state(y):
+        tt(R("t1"), R("sm"), PsE, OP.subtract)
+        tt(R("t1"), R("t1"), Pdp, OP.mult)
+        tt(PsE, PsE, R("t1"), OP.add)
+        tt(R("t2"), R(y), R("NCE"), OP.subtract)
+        tt(Pt, R("t2"), Pdp, OP.mult)
+        tt(R("NCE"), R("NCE"), Pt, OP.add)
+
+    def lanes_pre(t, between):
+        tt(R("key"), R("HB"), Pc, OP.add)
+        tree("key", L("keyv"), OP.min)
+        cp(R("keI"), L("keyv"))
+        ts(R("ceI"), R("keI"), 4095, OP.bitwise_and)
+        ts(L("full"), L("keyv"), 65536.0, OP.is_ge, 4096.0, OP.mult)
+        tt(L("x1"), R("ceI"), L("full"), OP.max)
+        cp(R("cl16"), L("x1"))
+        act(R("clOp"), IX(R("IW"), R("cl16")))
+        act(R("clR"), IX(R("clOp"), R("cur16")), bias=C(16))
+        act(R("decR"), IX(R("IW", 0, 8), R("dec16")), scale=-1.0)
+        act(R("OPW", 0, 256), R("ZB"))
+        act(R("LV"), IX(R("IW", 0, 256), R("cur16")), scale=C(2), bias=C(10 + t))
+        conv1("PSA", [("clR", 128, R("PKH"))])
+        ts(R("fkI"), R("keI"), 12, OP.arith_shift_right)
+        ts(L("fk1"), R("fkI"), 1.0, OP.add)
+        ts(R("acI"), R("wkI"), t, OP.arith_shift_right, 1, OP.bitwise_and)
+        cp(L("act"), R("acI"))
+        cp(R("COMP", 0, 48), R("DUM"))
+        between()
+        conv2("PSA", 0, "qh", "B8H")
+        tt(R("t4"), Pkb, R("HB"), OP.subtract)
+        tt(L("x2"), L("cur"), L("dm256"), OP.subtract)
+        cp(L("clS"), R("PSA", 0, 16))
+        ts(L("cl"), L("clS"), 2048.0, OP.add)
+        cp(R("lc16"), L("cl"))
+        act(R("G1"), IX(R("LK", 0, LW), R("lc16")), bias=C(17))
+
+    def judge(t):
+        tt(L("X"), R("code%d" % (t & 1)), R("lc%d" % t), OP.add)
+        ts(R("rdy"), L("X"), 0.0, OP.is_equal)
+        mm(R("PSR", 0, 16), R("B128"), R("rdy"), True, True)
+        mm(R("PSR", 16, 32), R("BTM"), R("rdy"), True, True)
+        conv1("PSA", [("G1", 128, R("PKP"))])
+        ts(R("cab", 16, 32), L("X"), 1.0, OP.is_ge)
+        tt(L("e"), L("dm256"), R("rdy"), OP.mult)
+        tt(L("e"), L("dm256"), L("e"), OP.subtract)
+        comp("v", [R("PSR", 0, 16), L("z")], [L("inc")],
+             lambda: g.vector.tensor_tensor_scan(ap(L("inc")), ap(R("PSR", 0, 16)), ap(L("z")), 0.0, OP.add, OP.add))
+        tt(L("rank"), R("PSR", 16, 32), L("inc"), OP.add)
+        ts(L("cm"), L("rank"), 48.0, OP.is_lt)
+        tt(R("cab", 0, 16), L("cm"), R("rdy"), OP.mult)
+        tt(L("done"), R("cab", 0, 16), R("cab", 16, 32), OP.add)
+        cp(R("dn16"), L("done"))
+        act(R("dnR"), IX(R("IW", 0, 8), R("dn16")))
+        act(R("gnR"), IX(R("dnR"), R("cur16")))
+        tt(L("x5"), L("rank"), R("rdy"), OP.mult)
+        tt(L("x5"), L("x5"), L("e"), OP.add)
+        cp(R("off16"), L("x5"))
+        conv2("PSA", 16, "q0")
+        for k in range(8):
+            mm(R("PSC", 16 * k, 16 * k + 16), R("ID"), R("cab", 0, 16), True, True)
+        for k in range(8):
+            mm(R("PSC", 128 + 16 * k, 144 + 16 * k), R("ID"), R("cab", 16, 32), True, True)
+        conv1("PSR", [("gnR", 128, R("PKP"))])
+        comp("v", [("n", "K", 0, 512, 1, 128), R("JC")], [IX(R("COMP"), R("off16"))],
+             lambda: g.vector.tensor_tensor(out=ap(IX(R("COMP"), R("off16"))), in0=T.K[:], in1=T.JC[:], op=OP.add))
+        cp(R("p16"), R("PSA", 16, 32))
+        cp(L("p"), R("p16"))
+        ts(R("Lt", 0, 24), R("COMP", 0, 24), C(2), OP.mult)
+        ts(R("Lt", 24, 48), R("COMP", 24, 48), C(1), OP.mult)
+        tt(R("Ls", 0, 24), R("Lt", 0, 24), R("Lt", 24, 48), OP.add)
+        ts(R("Ls", 24, 48), R("Ls", 0, 24), 2047, OP.bitwise_and)
+        cp(R("L16", 0, 24), R("Ls", 24, 48))
+        act(R("decL"), IX(R("decR"), R("p16")))
+        act(R("Dl"), IX(R("lb%d" % t), R("L16", 0, 24)))
+        conv1("PSA", [("G1", 128, R("PKO")), ("decL", 128, R("PKP"))])
+        ts(R("Ls", 48, 72), R("Ls", 0, 24), 11, OP.arith_shift_right)
+        cp(R("L16", 24, 48), R("Ls", 48, 72))
+        conv2("PSR", 32, "q1")
+        for c in range(16):
+            ts(R("EQ", 272 * c, 256 * c + 256), R("clR", 16 * c, 256), L("clS", c, c + 1), OP.is_equal)
+        conv2("PSA", 32, "q0")
+        ts(L("nf"), L("cl"), 4096.0, OP.is_lt)
+        tt(L("an"), L("act"), L("nf"), OP.mult)
+        tt(R("t3"), R("NCE"), Pc, OP.subtract)
+        ts(L("val"), R("PSA", 32, 48), 0.0, OP.is_gt)
+        tt(L("mv"), L("an"), L("val"), OP.mult)
+        tt(L("cand"), L("an"), L("mv"), OP.subtract)
+
+    def lanes_moves():
+        tt(L("x3"), L("cl"), L("dm4096"), OP.subtract)
+        tt(L("x1"), L("p"), L("cur"), OP.subtract)
+        tt(L("x1"), L("x1"), L("mv"), OP.mult)
+        tt(L("cur1"), L("cur"), L("x1"), OP.add)
+        tt(L("x4"), R("jW", 0, 16), L("cur1"), OP.subtract)
+        tt(L("x4"), L("x4"), R("PSR", 32, 48), OP.mult)
+
+    def new_cells(t):
+        tt(R("t1"), R("ln%d" % t), Pc, OP.subtract)
+        tt(R("t1"), R("t1"), R("PSC", 0, 128), OP.mult)
+        tt(R("t2"), R("t3"), R("PSC", 128, 256), OP.mult)
+        tt(Pc, Pc, R("t1"), OP.add)
+        tt(Pc, Pc, R("t2"), OP.add)
+        cp(R("c16"), Pc)
+
+    def commit_columns():
+        cp(IX(R("V", VB, E1), R("L16", 24, 48)), R("Dl"))
+
+    def masks():
+        cp(R("cmS"), R("PSC", 0, 128))
+        tt(Pdp, R("PSC", 128, 256), R("cmS"), OP.add)
+
+    def thresholds():
+        ts(R("t1"), Pdp, BIG, OP.mult, 150.0, OP.add)
+        tt(Pthr, PsE, R("t1"), OP.add)
+
+    def lanes_claim():
+        ts(L("x6"), R("PSR", 32, 48), -1.0, OP.mult, 1.0, OP.add)
+        tt(L("ac"), L("x6"), L("cand"), OP.mult)
+        tt(L("aw"), L("ac"), L("wW"), OP.mult)
+        for k in range(8):
+            ts(R("LH", 16 * k, 16 * k + 16), L("aw"), R("GC", k, k + 1), OP.mult)
+        for c in range(16):
+            mm(R("PSA", 16 * c, 256, 1, 8), R("LH", c, 128, 16), R("EQ", 272 * c, 256 * c + 256), c == 0, c == 15)
+
+    def lanes_out(t):
+        tt(L("win"), L("ac"), R("PSD", 0, 16), OP.mult)
+        tt(L("x1"), L("win"), L("x2"), OP.mult)
+        tt(L("x1"), L("x1"), L("dm256"), OP.add)
+        cp(R("oo16"), L("x1"))
+        cp(IX(R("OPW"), R("oo16")), R("ONE"))
+        conv1("PSD", [("OPW", 128, R("PKP"))])
+        lanes_moves()
+        conv2("PSD", 16, "q1")
+        if t < STEPS - 1:
+            tt(L("x5"), L("win"), L("x3"), OP.mult)
+            tt(L("x5"), L("x5"), L("dm4096"), OP.add)
+            cp(R("ol16"), L("x5"))
+            ts(L("x6"), L("n32"), -1.0, OP.mult, 0.25, OP.add)
+            tt(L("x6"), L("x6"), L("done"), OP.mult)
+            tt(L("n32a"), L("n32"), L("x6"), OP.add)
+            ts(L("x6"), L("done"), float(t + 2), OP.mult)
+            tt(L("dec"), L("dec"), L("x6"), OP.max)
+            cp(R("dec16"), L("dec"))
+            tt(L("cur"), L("cur1"), L("x4"), OP.add)
+            cp(R("cur16"), L("cur"))
+        else:
+            tt(L("cur"), L("cur1"), L("x4"), OP.add)
+
+    def holders():
+        tt(R("rw"), L("fk1"), R("PSD", 16, 32), OP.mult)
+        for k in range(8):
+            mm(R("PSD", 128 + 16 * k, 144 + 16 * k), R("ID"), R("rw"), True, True)
+
+    def holders2():
+        tt(Pt, R("t4"), Pdp, OP.mult)
+        tt(R("HB"), R("HB"), Pt, OP.add)
+        tt(R("t5"), R("PSD", 128, 256), R("kp1"), OP.is_equal)
+        ts(Pu, R("t5"), 65536.0, OP.mult)
+        tt(R("HB"), R("HB"), Pu, OP.add)
+
+    def snap_window():
+        if Ecur[0] == E0: return E0, E1, E1, "eaA", "ejA"
+        return VB, VE, E0, "eaB", "ejB"
+
+    def snap_index():
+        lo, hi, new, ea, ej = snap_window()
+        tt(R("t5"), R(ea), Pc, OP.add)
+        tt(Pt, R("t5"), Pdp, OP.mult)
+        tt(R("t5"), R(ej), Pt, OP.add)
+        cp(R("ei16"), R("t5"))
+
+    def snap_gather():
+        lo, hi, new, ea, ej = snap_window()
+        act(R("V", new, new + 2048), IX(R("V", lo, hi), R("ei16")))
+        Ecur[0] = new
+
+    def const_last():
+        cp(R("GC"), R("B128", 0, 128, 16))
+        for ea, ej, vb, eb in (("eaA", "ejA", VB - E0, 0), ("eaB", "ejB", 0, E1 - VB)):
+            ts(R(ej), R("jW"), float(eb), OP.add)
+            ts(R(ea), R("jW"), -1.0, OP.mult, float(vb - eb), OP.add)
+
+    lanes_pre(0, const_last)
+    for t in range(STEPS):
+        judge(t)
+        lanes_claim()
+        new_cells(t)
+        commit_columns()
+        if t == STEPS - 1: break
+        n = t + 1
+        gather_front(n, lambda: lanes_out(t))
+        list_table()
+        masks()
+        thresholds()
+        if t < STEPS - 2:
+            snap_index()
+            snap_gather()
+        if t == 0: act(R("SELW"), R("SEL2"), scale=C(8))
+        scatter_act(IX(R("LK", 0, 4352), R("ol16")), R("LV"))
+        flags_front()
+        ts(L("wo"), R("PSD", 16, 32), -1.0 / 32, OP.mult)
+        tt(L("n32"), L("n32a"), L("wo"), OP.add)
+        tt(R("code%d" % (n & 1)), L("tr"), L("n32"), OP.add)
+        out_send(n, "co", R("code%d" % (n & 1)))
+        holders()
+        hash_back("yI%d" % (n & 1))
+        out_send(n, "nc", R("yI%d" % (n & 1)))
+        holders2()
+        lanes_pre(n, lambda: renew_state("yI%d" % (n & 1)))
+    t = STEPS - 1
+    masks()
+
+    def weigh(a, b2):
+        for b in range(a, b2):
+            mm(R("PSP", 0, 256), R("SELW", 128 * b, 128 * b + 128), R("V", VB + 256 * b, VB + 256 * b + 256), b == 0, b == 15)
+
+    weigh(0, 3)
+    lanes_win()
+    conv2("PSD", 0, "q1")
+    cp(R("sm"), Pc)
+    dma("y", T.yc[:], T.sm[:], [("sm", 0, 128)], [])
+    weigh(3, 10)
+    lanes_out(t)
+    dma("s", T.yl[:], T.lane[:, _L["cur"]:_L["cur"] + 16], flat(L("cur")), [])
+    holders()
+    weigh(10, 16)
+    holders2()
+    ts(R("d1"), R("HB"), 65536.0, OP.is_ge)
+    dma("y", T.yh[:], T.d1[:], [("d1", 0, 128)], [])
+    cp(R("yso"), R("PSP", 0, 256))
+    dma("s", T.ys[:], T.yso[:], [("yso", 0, 256)], [])
+    for sem in sorted(cnt):
+        if known["g"].get(sem, 0) < cnt[sem]:
+            g.wait_ge(T.sem[sem], cnt[sem])

@@ -4,6 +4,7 @@ from concourse.mybir import AluOpType as OP, ActivationFunctionType as AF
 STEPS = 5
 E0, VB, DB, E1, VE = 0, 2048, 6144, 6528, 8576
 LW = 4112
+LAG = (2.5, 4.5, 6.0, 0.1, 0.15)
 
 SCRATCH = {
     "V": ("sbuf", [128, VE], "bfloat16"),
@@ -26,7 +27,7 @@ SCRATCH = {
     "dnR": ("sbuf", [128, 256], "bfloat16"), "gnR": ("sbuf", [128, 256], "bfloat16"), "winR": ("sbuf", [128, 256], "bfloat16"),
     "Dl": ("sbuf", [128, 384], "bfloat16"), "yso": ("sbuf", [128, 256], "float32"),
     "i1": ("sbuf", [128, 8], "int32"), "col": ("sbuf", [128, 32], "float32"), "GC": ("sbuf", [128, 8], "float32"),
-    "lane": ("sbuf", [128, 656], "float32"), "red": ("sbuf", [128, 128], "float32"),
+    "lane": ("sbuf", [128, 688], "float32"), "red": ("sbuf", [128, 128], "float32"),
     "code0": ("sbuf", [128, 16], "float32"), "code1": ("sbuf", [128, 16], "float32"),
     "rdy": ("sbuf", [128, 16], "bfloat16"), "rw": ("sbuf", [128, 16], "bfloat16"), "cab": ("sbuf", [128, 32], "bfloat16"),
     "Ls": ("sbuf", [128, 72], "int32"), "Lt": ("sbuf", [128, 48], "float32"), "L16": ("sbuf", [128, 48], "uint16"),
@@ -47,6 +48,9 @@ for _t in range(STEPS):
     SCRATCH["ln%d" % _t] = ("sbuf", [128, 128], "int32")
 for _n in ("PSP", "PSM", "PSC", "PSR", "PSA", "PSD", "V0", "V1"):
     SCRATCH[_n] = ("psum", [128, 512], "float32")
+PLACES = {"lane": 4, "q0": 3, "q1": 2, "t1": 3, "t2": 3, "t5": 3, "Pi": 2, "A": 2, "Bv": 2, "key": 2, "cl16": 2, "p16": 2}
+for _n in PLACES:
+    SCRATCH[_n] = (SCRATCH[_n][0], [128, SCRATCH[_n][1][1] * PLACES[_n]], SCRATCH[_n][2])
 
 MSG = ("b0", "b1", "co", "nc")
 SEMAPHORES = ["qv", "qs", "qt", "qg"] + ["d%d" % i for i in range(28)]
@@ -56,7 +60,7 @@ for _t in range(STEPS):
 
 _L = {}
 for _i, _n in enumerate("cur cl clS p act nf an mv cand ac aw wW dm256 dm4096 win cur1 x1 x2 x3 x4 x5 x6 X rank inc e cm done n32 n32a wo "
-                        "keyv full tr z lm fk1 dec val".split()):
+                        "keyv full tr z lm fk1 dec val nr lose".split()):
     _L[_n] = 16 * _i
 
 
@@ -106,7 +110,7 @@ def rank_program(g, core, T, topo):
         relay_program(g, core, T, topo)
         return
     Q = {"v": g.vector, "s": g.scalar, "t": g.tensor, "y": g.sync, "g": g}
-    width = {n: b[1][1] for n, b in SCRATCH.items()}
+    width = {n: b[1][1] // PLACES.get(n, 1) for n, b in SCRATCH.items()}
     ispsum = {n: b[0] == "psum" for n, b in SCRATCH.items()}
     hist = {}
     ops = []
@@ -145,7 +149,7 @@ def rank_program(g, core, T, topo):
             for k2, v2 in kn.items():
                 if known[q].get(k2, 0) < v2: known[q][k2] = v2
 
-    def track(q, reads, writes, kind):
+    def track(q, reads, writes):
         deps = set()
         acc = [(b, lo, hi, False) for b, lo, hi in reads] + [(b, lo, hi, True) for b, lo, hi in writes]
         for b, lo, hi, w in acc:
@@ -170,90 +174,195 @@ def rank_program(g, core, T, topo):
                 hist[b] = hl = [x for x in hl if not (ops[x[3]][0] == q and lo <= x[0] and x[1] <= hi and (w or not x[2]))]
             hl.append((lo, hi, w, d))
 
-    def comp(q, reads, writes, fn):
-        deps, acc = track(q, sum((flat(r) for r in reads), []), sum((flat(w) for w in writes), []), "c")
-        for w in writes:
-            if w[0] == "i":
-                acc = [(b, lo, hi, (wr and b != w[2][1])) for b, lo, hi, wr in acc]
-        need(q, deps)
-        sem = "q" + q
-        cnt[sem] = cnt.get(sem, 0) + 1
-        fn().then_inc(T.sem[sem], 1)
-        record(q, acc, sem, cnt[sem])
+    ver = {}
+
+    def res(s, w=False):
+        if not isinstance(s, tuple): return s
+        if s[0] == "i": return ("i", res(s[1]), res(s[2]))
+        b = s[1]
+        if b not in PLACES: return s
+        wd = width[b]
+        key = (b, s[2] // 16) if b == "lane" else b
+        if w and (s[3] - s[2] == (16 if b == "lane" else wd)): ver[key] = (ver.get(key, -1) + 1) % PLACES[b]
+        sh = ver.get(key, 0) * wd
+        return ("n", b, s[2] + sh, s[3] + sh, s[4], s[5])
+
+    recs = []
+    group = []
+    sent = {}
+
+    def wid(s):
+        if s[0] == "i": return 16 * (s[2][3] - s[2][2])
+        return (s[3] - s[2] + s[4] - 1) // s[4]
+
+    def short(s):
+        b = s[1][1] if s[0] == "i" else s[1]
+        return SCRATCH[b][2] in ("bfloat16", "float16", "uint16")
+
+    def span(q, kind, r, w):
+        out, n = w[0], wid(w[0])
+        cyc = n
+        if out[0] == "i": cyc = 3.8 * n
+        elif any(isinstance(x, tuple) and x[0] == "i" for x in r): cyc = 1.56 * n
+        elif q == "t": cyc = max(64, wid(r[1]))
+        elif kind == "tt": cyc = n if any(ispsum[x[1]] for x in r) else 2 * n
+        elif q == "g": cyc = 2 * n + 150
+        elif q == "v" and kind == "ts" and short(out) and all(short(x) for x in r[:1]): cyc = n / 2
+        return 1.2 * (max(64, cyc) * 0.00083 + (0.06 if q == "s" else 0.01))
+
+    def comp(q, reads, writes, fn, kind="ts"):
+        r = [res(x) for x in reads]
+        w = [res(x, True) for x in writes]
+        rd = sum((flat(x) for x in r), [])
+        wr = []
+        for x in w:
+            if x[0] == "i":
+                wr += flat(x[1]); rd += flat(x[2])
+            else:
+                wr += flat(x)
+        item = (rd, wr, lambda: fn(r, w))
+        if group: group[-1].append((item, span(q, kind, r, w)))
+        else: recs.append((q, [item], span(q, kind, r, w), "c", None))
+
+    def together(fn):
+        group.append([])
+        fn()
+        got = group.pop()
+        recs.append(("t", [x[0] for x in got], sum(x[1] for x in got), "c", None))
 
     def dma(q, out, in_, reads, writes):
-        deps, acc = track(q, reads, writes, "d")
-        need(q, deps)
-        sem = "d%d" % nd[0]; nd[0] += 1
-        Q[q].dma_start(out, in_).then_inc(T.sem[sem], 16)
-        cnt[sem] = 16
-        record(q, acc, sem, 16)
+        recs.append((q, [(reads, writes, lambda: Q[q].dma_start(out, in_))], 0.06, "d", 2.5))
+
+    def out_send(t, m, srcspec):
+        s = res(srcspec)
+        recs.append(("g", [(flat(s), [], lambda: (t, m, s))], 0.9, "r", None))
+        sent[(t, m)] = len(recs) - 1
+        recs.append(("net", [([], [landing(m, t)], None)], 0.0, "a", (t, m)))
+
+    def build():
+        n = len(recs)
+        pred = [set() for _ in range(n)]
+        old = {}
+        for i in range(n):
+            q = recs[i][0]
+            for rd, wr, _ in recs[i][1]:
+                for b, lo, hi, w in [(b, lo, hi, False) for b, lo, hi in rd] + [(b, lo, hi, True) for b, lo, hi in wr]:
+                    hl = old.setdefault(b, [])
+                    for lo2, hi2, w2, d in hl:
+                        if d != i and ((ispsum.get(b, False) and recs[d][0] != q) or (lo < hi2 and lo2 < hi and (w or w2))): pred[i].add(d)
+                    if w and not ispsum.get(b, False): hl[:] = [x for x in hl if not (lo <= x[0] and x[1] <= hi)]
+                    hl.append((lo, hi, w, i))
+            if recs[i][3] == "a": pred[i].add(sent[recs[i][4]])
+        succ = [[] for _ in range(n)]
+        for i in range(n):
+            for d in pred[i]: succ[d].append(i)
+
+        def lag(d, i):
+            if recs[d][3] == "d": return recs[d][4]
+            if recs[i][3] == "a":
+                t, m = recs[i][4]
+                if m[0] == "b": return LAG[2]
+                return LAG[0] if route(core, t, T, topo)[1][m] is None else LAG[1]
+            if recs[d][3] == "r": return 3.0
+            return LAG[3] if recs[d][0] == recs[i][0] else LAG[4]
+
+        prio = [0.0] * n
+        for i in range(n - 1, -1, -1):
+            prio[i] = recs[i][2] + max([lag(i, j) + prio[j] for j in succ[i]] + [0.0])
+        left = [len(p) for p in pred]
+        est = [0.0] * n
+        ready = {}
+        free = {}
+        for i in range(n):
+            if left[i] == 0: ready.setdefault(recs[i][0], []).append(i)
+        order = []
+        for _ in range(n):
+            best = None
+            for q, rl in ready.items():
+                if not rl: continue
+                t0 = max(free.get(q, 0.0), min(est[i] for i in rl))
+                if best is None or t0 < best[0]: best = (t0, q)
+            t0, q = best
+            i = max([x for x in ready[q] if est[x] <= t0 + 1e-9], key=lambda x: (prio[x], -x))
+            ready[q].remove(i)
+            order.append(i)
+            end = t0 + recs[i][2]
+            if q != "net": free[q] = end
+            for j in succ[i]:
+                est[j] = max(est[j], end + lag(i, j))
+                left[j] -= 1
+                if left[j] == 0: ready.setdefault(recs[j][0], []).append(j)
+        for i in order:
+            q, items, _, kind, x = recs[i]
+            for rd, wr, fn in items:
+                if kind == "a":
+                    sem = "a%s%d" % (x[1], x[0]); cnt[sem] = 8
+                    record("net", [(b, lo, hi, True) for b, lo, hi in wr], sem, 8)
+                    continue
+                deps, acc = track(q, rd, wr)
+                need(q, deps)
+                if kind == "r":
+                    t, m, s = fn()
+                    dst, via = route(core, t, T, topo)
+                    send(g, T, topo, core, dst if via[m] is None else via[m], m, t, ap(s))
+                    sem = "l%s%d" % (m, t); cnt[sem] = 8
+                elif kind == "d":
+                    sem = "d%d" % nd[0]; nd[0] += 1
+                    fn().then_inc(T.sem[sem], 16); cnt[sem] = 16
+                else:
+                    sem = "q" + q
+                    cnt[sem] = cnt.get(sem, 0) + 1
+                    fn().then_inc(T.sem[sem], 1)
+                record(q, acc, sem, cnt[sem])
 
     def tt(out, a, b, op):
-        comp("v", [a, b], [out], lambda: g.vector.tensor_tensor(out=ap(out), in0=ap(a), in1=ap(b), op=op))
+        comp("v", [a, b], [out], lambda r, w: g.vector.tensor_tensor(out=ap(w[0]), in0=ap(r[0]), in1=ap(r[1]), op=op), "tt")
 
     def ts(out, a, s1, op0, s2=None, op1=None):
-        x1 = ap(s1) if isinstance(s1, tuple) else s1
-        x2 = ap(s2) if isinstance(s2, tuple) else s2
-        if op1 is None:
-            comp("v", [a, s1], [out], lambda: g.vector.tensor_scalar(out=ap(out), in0=ap(a), scalar1=x1, scalar2=None, op0=op0))
-        else:
-            comp("v", [a, s1, s2], [out], lambda: g.vector.tensor_scalar(out=ap(out), in0=ap(a), scalar1=x1, scalar2=x2, op0=op0, op1=op1))
+        def call(r, w):
+            x1 = ap(r[1]) if isinstance(s1, tuple) else s1
+            x2 = ap(r[2]) if isinstance(s2, tuple) else s2
+            if op1 is None: return g.vector.tensor_scalar(out=ap(w[0]), in0=ap(r[0]), scalar1=x1, scalar2=None, op0=op0)
+            return g.vector.tensor_scalar(out=ap(w[0]), in0=ap(r[0]), scalar1=x1, scalar2=x2, op0=op0, op1=op1)
+        comp("v", [a, s1, s2], [out], call)
 
     def cp(out, a):
-        comp("v", [a], [out], lambda: g.vector.tensor_copy(out=ap(out), in_=ap(a)))
+        comp("v", [a], [out], lambda r, w: g.vector.tensor_copy(out=ap(w[0]), in_=ap(r[0])))
 
     def fill(out, x):
-        comp("v", [], [out], lambda: g.vector.memset(ap(out), x))
+        comp("v", [], [out], lambda r, w: g.vector.memset(ap(w[0]), x), "fill")
 
     def act(out, a, func=AF.Copy, scale=1.0, bias=None):
-        sc = ap(scale) if isinstance(scale, tuple) else scale
-        if bias is None:
-            comp("s", [a, scale], [out], lambda: g.scalar.activation(out=ap(out), in_=ap(a), func=func, scale=sc))
-        else:
-            comp("s", [a, scale, bias], [out], lambda: g.scalar.activation(out=ap(out), in_=ap(a), func=AF.Identity, bias=ap(bias), scale=sc))
+        def call(r, w):
+            sc = ap(r[1]) if isinstance(scale, tuple) else scale
+            if bias is None: return g.scalar.activation(out=ap(w[0]), in_=ap(r[0]), func=func, scale=sc)
+            return g.scalar.activation(out=ap(w[0]), in_=ap(r[0]), func=AF.Identity, bias=ap(r[2]), scale=sc)
+        comp("s", [a, scale, bias], [out], call)
 
     def scatter_act(out, a):
-        comp("s", [a], [out], lambda: g.scalar.activation(out=ap(out), in_=ap(a), func=AF.Silu))
+        comp("s", [a], [out], lambda r, w: g.scalar.activation(out=ap(w[0]), in_=ap(r[0]), func=AF.Silu))
 
     def mm(out, lhsT, rhs, start, stop):
-        comp("t", [lhsT, rhs], [out], lambda: g.tensor.matmul(ap(out), ap(lhsT), ap(rhs), start, stop))
+        comp("t", [lhsT, rhs], [out], lambda r, w: g.tensor.matmul(ap(w[0]), ap(r[0]), ap(r[1]), start, stop))
 
-    def iota(out, pattern, base, cm):
-        comp("g", [], [out], lambda: g.iota(ap(out), pattern, base, cm, allow_small_or_imprecise_dtypes=True))
+    def iota(out, pattern, base, cm, after=()):
+        comp("g", list(after), [out], lambda r, w: g.iota(ap(w[0]), pattern, base, cm, allow_small_or_imprecise_dtypes=True))
 
     def asel(out, a, pattern, op, base, cm):
-        comp("g", [a], [out], lambda: g.affine_select(ap(out), ap(a), pattern, op, 0.0, base, cm))
+        comp("g", [a], [out], lambda r, w: g.affine_select(ap(w[0]), ap(r[0]), pattern, op, 0.0, base, cm))
 
     def conv1(bank, parts):
-        for h in range(2):
-            for n, (src, np, pick) in enumerate(parts):
-                mm(R(bank, 256 + 128 * h, 384 + 128 * h), R(src, 128 * h, 128 * h + 128, 1, np), pick, n == 0, n == len(parts) - 1)
+        def run():
+            for h in range(2):
+                for n, (src, np, pick) in enumerate(parts):
+                    mm(R(bank, 256 + 128 * h, 384 + 128 * h), R(src, 128 * h, 128 * h + 128, 1, np), pick, n == 0, n == len(parts) - 1)
+        together(run)
 
     def conv2(bank, lo, q, b8="B8"):
         tt(R(q), R(bank, 256, 512), R("MK"), OP.mult)
-        for h in range(2):
-            mm(R(bank, lo + 8 * h, lo + 8 * h + 8), R(q, 128 * h, 128 * h + 128), R(b8), True, True)
-
-    def out_send(t, m, srcspec):
-        dst, via = route(core, t, T, topo)
-        to = dst if via[m] is None else via[m]
-        deps, acc = track("g", flat(srcspec), [], "r")
-        need("g", deps)
-        send(g, T, topo, core, to, m, t, ap(srcspec))
-        sem = "l%s%d" % (m, t)
-        cnt[sem] = 8
-        record("g", acc, sem, 8)
-
-    def arrive(t, m):
-        buf, lo, hi = landing(m, t)
-        sem = "a%s%d" % (m, t)
-        cnt[sem] = 8
-        record("net", [(buf, lo, hi, True)], sem, 8)
+        together(lambda: [mm(R(bank, lo + 8 * h, lo + 8 * h + 8), R(q, 128 * h, 128 * h + 128), R(b8), True, True) for h in range(2)])
 
     BIG = 1.0e6
-    for t in range(STEPS):
-        for m in MSG: arrive(t, m)
     Pc, PsE, Pdp, Pt = (R("V0", 128 * i, 128 * i + 128) for i in range(4))
     Pthr, Pk, Pkb, Pu = (R("V1", 128 * i, 128 * i + 128) for i in range(4))
 
@@ -268,11 +377,11 @@ def rank_program(g, core, T, topo):
     asel(R("B128"), R("BTM"), [[16, 8], [0, 16]], OP.is_ge, 15, -1)
     iota(R("kI"), [[1, 8], [0, 16]], 0, 0)
     iota(R("eaA"), [[16, 128]], 0, 0)
-    asel(R("q1", 0, 128), R("B128"), [[-1, 128]], OP.is_ge, 0, 1)
+    asel(R("BTM"), R("B128"), [[-1, 128]], OP.is_ge, 0, 1)
     asel(R("ID"), R("B128"), [[-1, 128]], OP.is_equal, 0, 1)
     iota(R("OR"), [[1, 256]], 0, 0)
     iota(R("clOp"), [[0, 16], [1, 16]], 0, 0)
-    iota(R("IW"), [[1, LW]], 0, 0)
+    iota(R("IW"), [[1, LW]], 0, 0, [R("ID"), R("clOp"), R("OR"), R("eaA"), R("kI")])
     fill(R("SEL2"), 0.0)
     for i in range(16):
         ts(R("SEL2", 129 * i, 128 * i + 128, 16), R("B128", i, 128, 16), 2.0, OP.mult)
@@ -306,8 +415,8 @@ def rank_program(g, core, T, topo):
     Ecur = [E0]
 
     def P_chunk(buf, lo, h):
-        for i in range(16):
-            mm(R("PSP", 64 * h, 64 * h + 64), R("SELPK", 128 * i, 128 * i + 128), R(buf, lo + 1024 * h + i, lo + 1024 * h + 1024, 16), i == 0, i == 15)
+        together(lambda: [mm(R("PSP", 64 * h, 64 * h + 64), R("SELPK", 128 * i, 128 * i + 128), R(buf, lo + 1024 * h + i, lo + 1024 * h + 1024, 16),
+                             i == 0, i == 15) for i in range(16)])
 
     def hash_front():
         cp(R("Pi"), R("PSP", 0, 128))
@@ -342,8 +451,8 @@ def rank_program(g, core, T, topo):
                 if t > 0: conv2("PSD", 0, "q1")
                 P_chunk(gt, 0, h)
                 between()
-            for i in range(16):
-                mm(R("PSM", 64 * h, 64 * h + 64), R("SEL2", 128 * i, 128 * i + 128), R("mx", 1024 * h + i, 1024 * h + 1024, 16), i == 0, i == 15)
+            together(lambda: [mm(R("PSM", 64 * h, 64 * h + 64), R("SEL2", 128 * i, 128 * i + 128), R("mx", 1024 * h + i, 1024 * h + 1024, 16),
+                                 i == 0, i == 15) for i in range(16)])
 
     def list_table():
         act(R("cR"), IX(R("IW", 0, 4096), R("c16")), scale=2048.0)
@@ -409,7 +518,7 @@ def rank_program(g, core, T, topo):
     ts(L("dm4096"), R("jW", 0, 16), 4096.0, OP.add)
     fill(L("z"), 0.0); fill(L("dec"), 0.0); fill(R("ZB"), 0.0)
     fill(R("V", DB, E1), 0.0)
-    ts(R("BTM"), R("q1", 0, 128), -1.0, OP.mult)
+    ts(R("BTM"), R("BTM"), -1.0, OP.mult)
     cp(R("dec16"), L("dec"))
 
     def renew_state(y):
@@ -438,11 +547,10 @@ def rank_program(g, core, T, topo):
         ts(L("fk1"), R("fkI"), 1.0, OP.add)
         ts(R("acI"), R("wkI"), t, OP.arith_shift_right, 1, OP.bitwise_and)
         cp(L("act"), R("acI"))
-        cp(R("COMP", 0, 48), R("DUM"))
+        act(R("COMP", 0, 48), R("DUM"))
         between()
         conv2("PSA", 0, "qh", "B8H")
         tt(R("t4"), Pkb, R("HB"), OP.subtract)
-        tt(L("x2"), L("cur"), L("dm256"), OP.subtract)
         cp(L("clS"), R("PSA", 0, 16))
         ts(L("cl"), L("clS"), 2048.0, OP.add)
         cp(R("lc16"), L("cl"))
@@ -451,14 +559,13 @@ def rank_program(g, core, T, topo):
     def judge(t):
         tt(L("X"), R("code%d" % (t & 1)), R("lc%d" % t), OP.add)
         ts(R("rdy"), L("X"), 0.0, OP.is_equal)
-        mm(R("PSR", 0, 16), R("B128"), R("rdy"), True, True)
-        mm(R("PSR", 16, 32), R("BTM"), R("rdy"), True, True)
+        together(lambda: [mm(R("PSR", 0, 16), R("B128"), R("rdy"), True, True), mm(R("PSR", 16, 32), R("BTM"), R("rdy"), True, True)])
         conv1("PSA", [("G1", 128, R("PKP"))])
         ts(R("cab", 16, 32), L("X"), 1.0, OP.is_ge)
-        tt(L("e"), L("dm256"), R("rdy"), OP.mult)
-        tt(L("e"), L("dm256"), L("e"), OP.subtract)
+        ts(L("nr"), L("X"), 0.0, OP.is_gt)
+        tt(L("e"), L("dm256"), L("nr"), OP.mult)
         comp("v", [R("PSR", 0, 16), L("z")], [L("inc")],
-             lambda: g.vector.tensor_tensor_scan(ap(L("inc")), ap(R("PSR", 0, 16)), ap(L("z")), 0.0, OP.add, OP.add))
+             lambda r, w: g.vector.tensor_tensor_scan(ap(w[0]), ap(r[0]), ap(r[1]), 0.0, OP.add, OP.add))
         tt(L("rank"), R("PSR", 16, 32), L("inc"), OP.add)
         ts(L("cm"), L("rank"), 48.0, OP.is_lt)
         tt(R("cab", 0, 16), L("cm"), R("rdy"), OP.mult)
@@ -466,17 +573,14 @@ def rank_program(g, core, T, topo):
         cp(R("dn16"), L("done"))
         act(R("dnR"), IX(R("IW", 0, 8), R("dn16")))
         act(R("gnR"), IX(R("dnR"), R("cur16")))
-        tt(L("x5"), L("rank"), R("rdy"), OP.mult)
-        tt(L("x5"), L("x5"), L("e"), OP.add)
+        tt(L("x5"), L("rank"), L("e"), OP.max)
         cp(R("off16"), L("x5"))
         conv2("PSA", 16, "q0")
-        for k in range(8):
-            mm(R("PSC", 16 * k, 16 * k + 16), R("ID"), R("cab", 0, 16), True, True)
-        for k in range(8):
-            mm(R("PSC", 128 + 16 * k, 144 + 16 * k), R("ID"), R("cab", 16, 32), True, True)
+        together(lambda: [mm(R("PSC", 128 * j + 16 * k, 128 * j + 16 * k + 16), R("ID"), R("cab", 16 * j, 16 * j + 16), True, True)
+                          for j in range(2) for k in range(8)])
         conv1("PSR", [("gnR", 128, R("PKP"))])
         comp("v", [("n", "K", 0, 512, 1, 128), R("JC")], [IX(R("COMP"), R("off16"))],
-             lambda: g.vector.tensor_tensor(out=ap(IX(R("COMP"), R("off16"))), in0=T.K[:], in1=T.JC[:], op=OP.add))
+             lambda r, w: g.vector.tensor_tensor(out=ap(w[0]), in0=T.K[:], in1=T.JC[:], op=OP.add))
         cp(R("p16"), R("PSA", 16, 32))
         cp(L("p"), R("p16"))
         ts(R("Lt", 0, 24), R("COMP", 0, 24), C(2), OP.mult)
@@ -501,7 +605,6 @@ def rank_program(g, core, T, topo):
         tt(L("cand"), L("an"), L("mv"), OP.subtract)
 
     def lanes_moves():
-        tt(L("x3"), L("cl"), L("dm4096"), OP.subtract)
         tt(L("x1"), L("p"), L("cur"), OP.subtract)
         tt(L("x1"), L("x1"), L("mv"), OP.mult)
         tt(L("cur1"), L("cur"), L("x1"), OP.add)
@@ -533,21 +636,21 @@ def rank_program(g, core, T, topo):
         tt(L("aw"), L("ac"), L("wW"), OP.mult)
         for k in range(8):
             ts(R("LH", 16 * k, 16 * k + 16), L("aw"), R("GC", k, k + 1), OP.mult)
-        for c in range(16):
-            mm(R("PSA", 16 * c, 256, 1, 8), R("LH", c, 128, 16), R("EQ", 272 * c, 256 * c + 256), c == 0, c == 15)
+        together(lambda: [mm(R("PSA", 16 * c, 256, 1, 8), R("LH", c, 128, 16), R("EQ", 272 * c, 256 * c + 256), c == 0, c == 15) for c in range(16)])
 
     def lanes_out(t):
         tt(L("win"), L("ac"), R("PSD", 0, 16), OP.mult)
-        tt(L("x1"), L("win"), L("x2"), OP.mult)
-        tt(L("x1"), L("x1"), L("dm256"), OP.add)
+        ts(L("lose"), L("win"), -1.0, OP.mult, 1.0, OP.add)
+        tt(L("x1"), L("lose"), L("dm256"), OP.mult)
+        tt(L("x1"), L("x1"), L("cur"), OP.max)
         cp(R("oo16"), L("x1"))
         cp(IX(R("OPW"), R("oo16")), R("ONE"))
         conv1("PSD", [("OPW", 128, R("PKP"))])
         lanes_moves()
         conv2("PSD", 16, "q1")
         if t < STEPS - 1:
-            tt(L("x5"), L("win"), L("x3"), OP.mult)
-            tt(L("x5"), L("x5"), L("dm4096"), OP.add)
+            tt(L("x5"), L("lose"), L("dm4096"), OP.mult)
+            tt(L("x5"), L("x5"), L("cl"), OP.max)
             cp(R("ol16"), L("x5"))
             ts(L("x6"), L("n32"), -1.0, OP.mult, 0.25, OP.add)
             tt(L("x6"), L("x6"), L("done"), OP.mult)
@@ -562,8 +665,7 @@ def rank_program(g, core, T, topo):
 
     def holders():
         tt(R("rw"), L("fk1"), R("PSD", 16, 32), OP.mult)
-        for k in range(8):
-            mm(R("PSD", 128 + 16 * k, 144 + 16 * k), R("ID"), R("rw"), True, True)
+        together(lambda: [mm(R("PSD", 128 + 16 * k, 144 + 16 * k), R("ID"), R("rw"), True, True) for k in range(8)])
 
     def holders2():
         tt(Pt, R("t4"), Pdp, OP.mult)
@@ -635,7 +737,8 @@ def rank_program(g, core, T, topo):
     dma("y", T.yc[:], T.sm[:], [("sm", 0, 128)], [])
     weigh(3, 10)
     lanes_out(t)
-    dma("s", T.yl[:], T.lane[:, _L["cur"]:_L["cur"] + 16], flat(L("cur")), [])
+    last = res(L("cur"))
+    dma("s", T.yl[:], ap(last), flat(last), [])
     holders()
     weigh(10, 16)
     holders2()
@@ -643,6 +746,7 @@ def rank_program(g, core, T, topo):
     dma("y", T.yh[:], T.d1[:], [("d1", 0, 128)], [])
     cp(R("yso"), R("PSP", 0, 256))
     dma("s", T.ys[:], T.yso[:], [("yso", 0, 256)], [])
+    build()
     for sem in sorted(cnt):
         if known["g"].get(sem, 0) < cnt[sem]:
             g.wait_ge(T.sem[sem], cnt[sem])

import math
from concourse.mybir import AluOpType as OP, ActivationFunctionType as AF

STEPS = 5
E0, VB, DB, E1, VE = 0, 2048, 6144, 6528, 8576
LW = 4112
LAG = (2.5, 4.5, 6.0, 0.1, 0.15)

SCRATCH = {
    "V": ("sbuf", [128, VE], "bfloat16"),
    "got0": ("sbuf", [128, 2048], "bfloat16"), "got1": ("sbuf", [128, 2048], "bfloat16"),
    "mx": ("sbuf", [128, 2048], "bfloat16"), "cR": ("sbuf", [128, 2048], "float32"),
    "IW": ("sbuf", [128, LW], "float32"), "LK": ("sbuf", [128, 6144], "float32"),
    "LV0": ("sbuf", [128, 2048], "float32"), "LV": ("sbuf", [128, 256], "float32"),
    "SEL2": ("sbuf", [128, 2048], "bfloat16"), "SELPK": ("sbuf", [128, 2048], "bfloat16"), "SELW": ("sbuf", [128, 2048], "bfloat16"),
    "MK": ("sbuf", [128, 256], "bfloat16"), "PKP": ("sbuf", [128, 128], "bfloat16"), "PKO": ("sbuf", [128, 128], "bfloat16"),
    "PKH": ("sbuf", [128, 128], "float16"), "PK8": ("sbuf", [128, 128], "bfloat16"),
    "B8": ("sbuf", [128, 8], "bfloat16"), "B8H": ("sbuf", [128, 8], "float16"),
    "q0": ("sbuf", [128, 256], "bfloat16"), "q1": ("sbuf", [128, 256], "bfloat16"), "qh": ("sbuf", [128, 256], "float16"),
    "EQ": ("sbuf", [128, 4096], "bfloat16"), "LH": ("sbuf", [128, 128], "bfloat16"),
    "ONE": ("sbuf", [128, 256], "bfloat16"), "ZB": ("sbuf", [128, 256], "bfloat16"), "OPW": ("sbuf", [128, 512], "bfloat16"),
    "B128": ("sbuf", [128, 128], "bfloat16"), "BTM": ("sbuf", [128, 128], "bfloat16"), "ID": ("sbuf", [128, 128], "bfloat16"),
    "OR": ("sbuf", [128, 256], "float32"), "JC": ("sbuf", [128, 256], "float32"), "K": ("sbuf", [128, 256], "float32"),
    "COMP": ("sbuf", [128, 512], "float32"), "DUM": ("sbuf", [128, 48], "float32"), "thrR": ("sbuf", [128, 256], "float32"),
    "clOp": ("sbuf", [128, 256], "float32"), "clR": ("sbuf", [128, 256], "float16"),
    "G1": ("sbuf", [128, 256], "bfloat16"), "decR": ("sbuf", [128, 256], "bfloat16"), "decL": ("sbuf", [128, 256], "bfloat16"),
    "dnR": ("sbuf", [128, 256], "bfloat16"), "gnR": ("sbuf", [128, 256], "bfloat16"), "winR": ("sbuf", [128, 256], "bfloat16"),
    "Dl": ("sbuf", [128, 384], "bfloat16"), "yso": ("sbuf", [128, 256], "float32"),
    "i1": ("sbuf", [128, 8], "int32"), "col": ("sbuf", [128, 32], "float32"), "GC": ("sbuf", [128, 8], "float32"),
    "lane": ("sbuf", [128, 688], "float32"), "red": ("sbuf", [128, 128], "float32"),
    "code0": ("sbuf", [128, 16], "float32"), "code1": ("sbuf", [128, 16], "float32"),
    "rdy": ("sbuf", [128, 16], "bfloat16"), "rw": ("sbuf", [128, 16], "bfloat16"), "cab": ("sbuf", [128, 32], "bfloat16"),
    "Ls": ("sbuf", [128, 72], "int32"), "Lt": ("sbuf", [128, 48], "float32"), "L16": ("sbuf", [128, 48], "uint16"),
}
for _n in ("csI", "hdI", "kI", "Pi", "A", "Bv", "pr", "h", "yI0", "yI1"):
    SCRATCH[_n] = ("sbuf", [128, 128], "int32")
for _n in ("HB", "kp1", "NCE", "sm", "d1", "bd", "cmS", "key", "jW", "eaA", "ejA", "eaB", "ejB", "t1", "t2", "t3", "t4", "t5"):
    SCRATCH[_n] = ("sbuf", [128, 128], "float32")
for _n in ("c16", "ei16"):
    SCRATCH[_n] = ("sbuf", [128, 128], "uint16")
for _n in ("wkI", "keI", "ceI", "fkI", "acI"):
    SCRATCH[_n] = ("sbuf", [128, 16], "int32")
for _n in ("cl16", "cur16", "lc16", "p16", "dn16", "off16", "oo16", "ol16", "dec16"):
    SCRATCH[_n] = ("sbuf", [128, 16], "uint16")
for _t in range(STEPS):
    SCRATCH["lb%d" % _t] = ("sbuf", [128, 2048], "bfloat16")
    SCRATCH["lc%d" % _t] = ("sbuf", [128, 16], "float32")
    SCRATCH["ln%d" % _t] = ("sbuf", [128, 128], "int32")
for _n in ("PSP", "PSM", "PSC", "PSR", "PSA", "PSD", "V0", "V1"):
    SCRATCH[_n] = ("psum", [128, 512], "float32")
PLACES = {"lane": 4, "q0": 3, "q1": 2, "t1": 3, "t2": 3, "t5": 3, "Pi": 2, "A": 2, "Bv": 2, "key": 2, "cl16": 2, "p16": 2}
for _n in PLACES:
    SCRATCH[_n] = (SCRATCH[_n][0], [128, SCRATCH[_n][1][1] * PLACES[_n]], SCRATCH[_n][2])

MSG = ("b0", "b1", "co", "nc")
SEMAPHORES = ["qv", "qs", "qt", "qg"] + ["d%d" % i for i in range(28)]
for _t in range(STEPS):
    for _m in MSG:
        SEMAPHORES += ["a%s%d" % (_m, _t), "l%s%d" % (_m, _t)]

_L = {}
for _i, _n in enumerate("cur cl clS p act nf an mv cand ac aw wW dm256 dm4096 win cur1 x1 x2 x3 x4 x5 x6 X rank inc e cm done n32 n32a wo "
                        "keyv full tr z lm fk1 dec val nr lose".split()):
    _L[_n] = 16 * _i


def landing(m, t):
    if m == "b0": return "lb%d" % t, 0, 1024
    if m == "b1": return "lb%d" % t, 1024, 2048
    if m == "co": return "lc%d" % t, 0, 16
    return "ln%d" % t, 0, 128


def route(core, t, T, topo):
    dst = T.cores[T.rank_of(core) ^ (1 + t % 7)]
    near = [x for x in topo.cores_of(core) if x != core and topo.die(x) == topo.die(core) and topo.may_write(x, dst)]
    far = [x for x in topo.cores_of(core) if topo.die(x) != topo.die(core) and topo.may_write(x, dst)]
    via = {"b0": near[-1], "b1": near[-2], "co": None, "nc": None}
    if not topo.may_write(core, dst):
        via["co"] = far[0]; via["nc"] = far[1]
    return dst, via


def engines8(topo, a, b):
    return sum(1 << e for e in topo.engines(a, b)[:8])


def send(g, T, topo, core, dst, m, t, src):
    buf, lo, hi = landing(m, t)
    rid, pid = topo.addr(dst, core)
    return g.remote_dma(out_ap=T[buf][:, lo:hi], in_ap=src, remote_sem=T.sem["a%s%d" % (m, t)], local_sem=T.sem["l%s%d" % (m, t)],
                        pid=pid, routing_id=rid, dma_engine_mask=engines8(topo, core, dst))


def relay_program(g, core, T, topo):
    for src in [x for x in topo.cores_of(core) if T.rank_of(x) is not None]:
        for t in range(STEPS):
            dst, via = route(src, t, T, topo)
            mine = [m for m in MSG if via[m] == core]
            for m in mine:
                buf, lo, hi = landing(m, t)
                g.wait_ge(T.sem["a%s%d" % (m, t)], 8)
                send(g, T, topo, core, dst, m, t, T[buf][:, lo:hi])
            for m in mine:
                g.wait_ge(T.sem["l%s%d" % (m, t)], 8)


def rank_program(g, core, T, topo):
    if T.rank_of(core) is None:
        relay_program(g, core, T, topo)
        return
    Q = {"v": g.vector, "s": g.scalar, "t": g.tensor, "y": g.sync, "g": g}
    width = {n: b[1][1] // PLACES.get(n, 1) for n, b in SCRATCH.items()}
    ispsum = {n: b[0] == "psum" for n, b in SCRATCH.items()}
    hist = {}
    ops = []
    known = {q: {} for q in Q}
    cnt = {}
    nd = [0]

    def R(b, lo=0, hi=None, st=1, np=128):
        return ("n", b, lo, width[b] if hi is None else hi, st, np)

    def L(n, a=0, b=16):
        return ("n", "lane", _L[n] + a, _L[n] + b, 1, 128)

    def C(i):
        return ("n", "col", i, i + 1, 1, 128)

    def IX(w, o):
        return ("i", w, o)

    def ap(s):
        if s[0] == "i": return ap(s[1]).indirect(ap(s[2]))
        p = slice(0, s[5]) if s[5] < 128 else slice(None)
        if s[4] == 1: return T[s[1]][p, s[2]:s[3]]
        return T[s[1]][p, s[2]:s[3]:s[4]]

    def flat(s):
        if not isinstance(s, tuple): return []
        if s[0] == "i": return flat(s[1]) + flat(s[2])
        return [(s[1], s[2], s[3])]

    def need(q, deps):
        for d in sorted(deps, reverse=True):
            _, sem, n, kn = ops[d]
            if known[q].get(sem, 0) >= n: continue
            Q[q].wait_ge(T.sem[sem], n)
            for k2, v2 in kn.items():
                if known[q].get(k2, 0) < v2: known[q][k2] = v2

    def track(q, reads, writes):
        deps = set()
        acc = [(b, lo, hi, False) for b, lo, hi in reads] + [(b, lo, hi, True) for b, lo, hi in writes]
        for b, lo, hi, w in acc:
            for lo2, hi2, w2, d in hist.get(b, ()):
                meet = lo < hi2 and lo2 < hi and (w or w2)
                if ispsum.get(b, False):
                    if ops[d][0] != q or (q != "t" and meet): deps.add(d)
                elif meet:
                    deps.add(d)
        return deps, acc

    def record(q, acc, sem, n):
        kn = dict(known[q]) if q in known else {}
        kn[sem] = n
        ops.append((q, sem, n, kn))
        d = len(ops) - 1
        for b, lo, hi, w in acc:
            hl = hist.setdefault(b, [])
            if w and not ispsum.get(b, False):
                hist[b] = hl = [x for x in hl if not (lo <= x[0] and x[1] <= hi)]
            elif ispsum.get(b, False):
                hist[b] = hl = [x for x in hl if not (ops[x[3]][0] == q and lo <= x[0] and x[1] <= hi and (w or not x[2]))]
            hl.append((lo, hi, w, d))

    ver = {}

    def res(s, w=False):
        if not isinstance(s, tuple): return s
        if s[0] == "i": return ("i", res(s[1]), res(s[2]))
        b = s[1]
        if b not in PLACES: return s
        wd = width[b]
        key = (b, s[2] // 16) if b == "lane" else b
        if w and (s[3] - s[2] == (16 if b == "lane" else wd)): ver[key] = (ver.get(key, -1) + 1) % PLACES[b]
        sh = ver.get(key, 0) * wd
        return ("n", b, s[2] + sh, s[3] + sh, s[4], s[5])

    recs = []
    group = []
    sent = {}

    def wid(s):
        if s[0] == "i": return 16 * (s[2][3] - s[2][2])
        return (s[3] - s[2] + s[4] - 1) // s[4]

    def short(s):
        b = s[1][1] if s[0] == "i" else s[1]
        return SCRATCH[b][2] in ("bfloat16", "float16", "uint16")

    def span(q, kind, r, w):
        out, n = w[0], wid(w[0])
        cyc = n
        if out[0] == "i": cyc = 3.8 * n
        elif any(isinstance(x, tuple) and x[0] == "i" for x in r): cyc = 1.56 * n
        elif q == "t": cyc = max(64, wid(r[1]))
        elif kind == "tt": cyc = n if any(ispsum[x[1]] for x in r) else 2 * n
        elif q == "g": cyc = 2 * n + 150
        elif q == "v" and kind == "ts" and short(out) and all(short(x) for x in r[:1]): cyc = n / 2
        return 1.2 * (max(64, cyc) * 0.00083 + (0.06 if q == "s" else 0.01))

    def comp(q, reads, writes, fn, kind="ts"):
        r = [res(x) for x in reads]
        w = [res(x, True) for x in writes]
        rd = sum((flat(x) for x in r), [])
        wr = []
        for x in w:
            if x[0] == "i":
                wr += flat(x[1]); rd += flat(x[2])
            else:
                wr += flat(x)
        item = (rd, wr, lambda: fn(r, w))
        if group: group[-1].append((item, span(q, kind, r, w)))
        else: recs.append((q, [item], span(q, kind, r, w), "c", None))

    def together(fn):
        group.append([])
        fn()
        got = group.pop()
        recs.append(("t", [x[0] for x in got], sum(x[1] for x in got), "c", None))

    def dma(q, out, in_, reads, writes):
        recs.append((q, [(reads, writes, lambda: Q[q].dma_start(out, in_))], 0.06, "d", 2.5))

    def out_send(t, m, srcspec):
        s = res(srcspec)
        recs.append(("g", [(flat(s), [], lambda: (t, m, s))], 0.9, "r", None))
        sent[(t, m)] = len(recs) - 1
        recs.append(("net", [([], [landing(m, t)], None)], 0.0, "a", (t, m)))

    def build():
        n = len(recs)
        pred = [set() for _ in range(n)]
        old = {}
        for i in range(n):
            q = recs[i][0]
            for rd, wr, _ in recs[i][1]:
                for b, lo, hi, w in [(b, lo, hi, False) for b, lo, hi in rd] + [(b, lo, hi, True) for b, lo, hi in wr]:
                    hl = old.setdefault(b, [])
                    for lo2, hi2, w2, d in hl:
                        if d != i and ((ispsum.get(b, False) and recs[d][0] != q) or (lo < hi2 and lo2 < hi and (w or w2))): pred[i].add(d)
                    if w and not ispsum.get(b, False): hl[:] = [x for x in hl if not (lo <= x[0] and x[1] <= hi)]
                    hl.append((lo, hi, w, i))
            if recs[i][3] == "a": pred[i].add(sent[recs[i][4]])
        succ = [[] for _ in range(n)]
        for i in range(n):
            for d in pred[i]: succ[d].append(i)

        def lag(d, i):
            if recs[d][3] == "d": return recs[d][4]
            if recs[i][3] == "a":
                t, m = recs[i][4]
                if m[0] == "b": return LAG[2]
                return LAG[0] if route(core, t, T, topo)[1][m] is None else LAG[1]
            if recs[d][3] == "r": return 3.0
            return LAG[3] if recs[d][0] == recs[i][0] else LAG[4]

        prio = [0.0] * n
        for i in range(n - 1, -1, -1):
            prio[i] = recs[i][2] + max([lag(i, j) + prio[j] for j in succ[i]] + [0.0])
        left = [len(p) for p in pred]
        est = [0.0] * n
        ready = {}
        free = {}
        for i in range(n):
            if left[i] == 0: ready.setdefault(recs[i][0], []).append(i)
        order = []
        for _ in range(n):
            best = None
            for q, rl in ready.items():
                if not rl: continue
                t0 = max(free.get(q, 0.0), min(est[i] for i in rl))
                if best is None or t0 < best[0]: best = (t0, q)
            t0, q = best
            i = max([x for x in ready[q] if est[x] <= t0 + 1e-9], key=lambda x: (prio[x], -x))
            ready[q].remove(i)
            order.append(i)
            end = t0 + recs[i][2]
            if q != "net": free[q] = end
            for j in succ[i]:
                est[j] = max(est[j], end + lag(i, j))
                left[j] -= 1
                if left[j] == 0: ready.setdefault(recs[j][0], []).append(j)
        for i in order:
            q, items, _, kind, x = recs[i]
            for rd, wr, fn in items:
                if kind == "a":
                    sem = "a%s%d" % (x[1], x[0]); cnt[sem] = 8
                    record("net", [(b, lo, hi, True) for b, lo, hi in wr], sem, 8)
                    continue
                deps, acc = track(q, rd, wr)
                need(q, deps)
                if kind == "r":
                    t, m, s = fn()
                    dst, via = route(core, t, T, topo)
                    send(g, T, topo, core, dst if via[m] is None else via[m], m, t, ap(s))
                    sem = "l%s%d" % (m, t); cnt[sem] = 8
                elif kind == "d":
                    sem = "d%d" % nd[0]; nd[0] += 1
                    fn().then_inc(T.sem[sem], 16); cnt[sem] = 16
                else:
                    sem = "q" + q
                    cnt[sem] = cnt.get(sem, 0) + 1
                    fn().then_inc(T.sem[sem], 1)
                record(q, acc, sem, cnt[sem])

    def tt(out, a, b, op):
        comp("v", [a, b], [out], lambda r, w: g.vector.tensor_tensor(out=ap(w[0]), in0=ap(r[0]), in1=ap(r[1]), op=op), "tt")

    def ts(out, a, s1, op0, s2=None, op1=None):
        def call(r, w):
            x1 = ap(r[1]) if isinstance(s1, tuple) else s1
            x2 = ap(r[2]) if isinstance(s2, tuple) else s2
            if op1 is None: return g.vector.tensor_scalar(out=ap(w[0]), in0=ap(r[0]), scalar1=x1, scalar2=None, op0=op0)
            return g.vector.tensor_scalar(out=ap(w[0]), in0=ap(r[0]), scalar1=x1, scalar2=x2, op0=op0, op1=op1)
        comp("v", [a, s1, s2], [out], call)

    def cp(out, a):
        comp("v", [a], [out], lambda r, w: g.vector.tensor_copy(out=ap(w[0]), in_=ap(r[0])))

    def fill(out, x):
        comp("v", [], [out], lambda r, w: g.vector.memset(ap(w[0]), x), "fill")

    def act(out, a, func=AF.Copy, scale=1.0, bias=None):
        def call(r, w):
            sc = ap(r[1]) if isinstance(scale, tuple) else scale
            if bias is None: return g.scalar.activation(out=ap(w[0]), in_=ap(r[0]), func=func, scale=sc)
            return g.scalar.activation(out=ap(w[0]), in_=ap(r[0]), func=AF.Identity, bias=ap(r[2]), scale=sc)
        comp("s", [a, scale, bias], [out], call)

    def scatter_act(out, a):
        comp("s", [a], [out], lambda r, w: g.scalar.activation(out=ap(w[0]), in_=ap(r[0]), func=AF.Silu))

    def mm(out, lhsT, rhs, start, stop):
        comp("t", [lhsT, rhs], [out], lambda r, w: g.tensor.matmul(ap(w[0]), ap(r[0]), ap(r[1]), start, stop))

    def iota(out, pattern, base, cm, after=()):
        comp("g", list(after), [out], lambda r, w: g.iota(ap(w[0]), pattern, base, cm, allow_small_or_imprecise_dtypes=True))

    def asel(out, a, pattern, op, base, cm):
        comp("g", [a], [out], lambda r, w: g.affine_select(ap(w[0]), ap(r[0]), pattern, op, 0.0, base, cm))

    def conv1(bank, parts):
        def run():
            for h in range(2):
                for n, (src, np, pick) in enumerate(parts):
                    mm(R(bank, 256 + 128 * h, 384 + 128 * h), R(src, 128 * h, 128 * h + 128, 1, np), pick, n == 0, n == len(parts) - 1)
        together(run)

    def conv2(bank, lo, q, b8="B8"):
        tt(R(q), R(bank, 256, 512), R("MK"), OP.mult)
        together(lambda: [mm(R(bank, lo + 8 * h, lo + 8 * h + 8), R(q, 128 * h, 128 * h + 128), R(b8), True, True) for h in range(2)])

    BIG = 1.0e6
    Pc, PsE, Pdp, Pt = (R("V0", 128 * i, 128 * i + 128) for i in range(4))
    Pthr, Pk, Pkb, Pu = (R("V1", 128 * i, 128 * i + 128) for i in range(4))

    dma("y", T.csI[:], T.cs[:], [], [("csI", 0, 128)])
    dma("y", T.hdI[:], T.hold[:], [], [("hdI", 0, 128)])
    dma("y", T.V[:, VB:DB], T.x[:], [], [("V", VB, DB)])
    dma("y", T.V[:, E0:E0 + 2048], T.snap[:], [], [("V", E0, E0 + 2048)])
    dma("y", T.wkI[:], T.wake[:], [], [("wkI", 0, 16)])
    fill(R("ONE"), 1.0)
    iota(R("i1", 0, 1), [[0, 1]], 0, 1)
    asel(R("BTM"), R("ONE", 0, 128), [[-16, 8], [0, 16]], OP.is_ge, 0, 1)
    asel(R("B128"), R("BTM"), [[16, 8], [0, 16]], OP.is_ge, 15, -1)
    iota(R("kI"), [[1, 8], [0, 16]], 0, 0)
    iota(R("eaA"), [[16, 128]], 0, 0)
    asel(R("BTM"), R("B128"), [[-1, 128]], OP.is_ge, 0, 1)
    asel(R("ID"), R("B128"), [[-1, 128]], OP.is_equal, 0, 1)
    iota(R("OR"), [[1, 256]], 0, 0)
    iota(R("clOp"), [[0, 16], [1, 16]], 0, 0)
    iota(R("IW"), [[1, LW]], 0, 0, [R("ID"), R("clOp"), R("OR"), R("eaA"), R("kI")])
    fill(R("SEL2"), 0.0)
    for i in range(16):
        ts(R("SEL2", 129 * i, 128 * i + 128, 16), R("B128", i, 128, 16), 2.0, OP.mult)
    ts(R("i1", 1, 2), R("i1", 0, 1), 15, OP.bitwise_and)
    ts(R("i1", 2, 3), R("i1", 0, 1), 1, OP.bitwise_and)
    ts(R("i1", 3, 4), R("i1", 1, 2), 1, OP.arith_shift_right)
    cp(C(0), R("i1", 1, 2))
    cp(C(1), R("i1", 2, 3))
    ts(C(2), C(1), -1.0, OP.mult, 1.0, OP.add)
    ts(C(3), R("i1", 3, 4), 256.0, OP.mult)
    ts(C(4), C(0), 8.0, OP.is_lt, 0.5 - 1024.0, OP.mult)
    ts(C(5), C(4), 1024.0, OP.add)
    ts(C(9), C(1), 64.0, OP.add)
    ts(R("SELPK"), R("SEL2"), C(5), OP.mult)
    cp(Pk, R("kI"))
    ts(R("jW"), R("eaA"), C(0), OP.add)
    ts(R("t5"), R("jW"), 4096.0, OP.add)
    cp(Pc, R("csI"))
    cp(R("c16"), Pc)
    ts(R("LV0", 0, 256), R("OR"), C(2), OP.mult, C(9), OP.add)
    cp(R("t1"), R("hdI"))
    tt(R("t3"), Pc, R("t5"), OP.subtract)
    tt(R("t3"), R("t3"), R("t1"), OP.mult)
    tt(R("t3"), R("t3"), R("t5"), OP.add)
    cp(R("ei16"), R("t3"))
    cp(R("LV0", 256, 512), R("LV0", 0, 256))
    cp(R("LV0", 512, 1024), R("LV0", 0, 512))
    cp(R("LV0", 1024, 2048), R("LV0", 0, 1024))
    fill(R("LK", 0, LW), 0.0)

    Ecur = [E0]

    def P_chunk(buf, lo, h):
        together(lambda: [mm(R("PSP", 64 * h, 64 * h + 64), R("SELPK", 128 * i, 128 * i + 128), R(buf, lo + 1024 * h + i, lo + 1024 * h + 1024, 16),
                             i == 0, i == 15) for i in range(16)])

    def hash_front():
        cp(R("Pi"), R("PSP", 0, 128))
        ts(R("A"), R("Pi"), 2047, OP.bitwise_and)
        ts(R("Bv"), R("Pi"), 11, OP.arith_shift_right)
        tt(R("sm"), R("A"), R("Bv"), OP.add)

    def hash_back(y):
        tt(R("pr"), R("A"), R("Bv"), OP.mult)
        ts(R("h", 0, 16), R("pr", 0, 16), 3, OP.arith_shift_right, 4095, OP.bitwise_and)
        ts(R("h", 16, 128), R("pr", 16, 128), 3, OP.arith_shift_right, 511, OP.bitwise_and)
        for k in range(1, 8):
            tt(R("h", 16 * k, 16 * k + 16), R("h", 16 * k, 16 * k + 16), R("h", 16 * k - 16, 16 * k), OP.add)
        tt(R(y), R("h"), Pk, OP.add)
        ts(R(y), R(y), 4095, OP.bitwise_and)

    def lanes_win():
        tt(R("winR", 0, 256, 1, 8), R("PSA", 0, 256, 1, 8), R("thrR", 0, 256, 1, 8), OP.is_le)
        conv1("PSD", [("winR", 8, R("PK8", 0, 128, 1, 8))])

    def gather_front(t, between):
        gt = "got%d" % (t & 1)
        for h in range(2):
            lo = 1024 * h
            if h == 1 and t > 0: lanes_win()
            act(R(gt, lo, lo + 1024), IX(R("V", VB, DB), R("c16", 64 * h, 64 * h + 64)))
            tt(R("mx", lo, lo + 1024), IX(R("V", VB, DB), R("c16", 64 * h, 64 * h + 64)), R("V", Ecur[0] + lo, Ecur[0] + lo + 1024), OP.max)
            out_send(t, "b%d" % h, R(gt, lo, lo + 1024))
            if h == 0: P_chunk(gt, 0, h)
        for h in range(2):
            if h == 1:
                if t > 0: conv2("PSD", 0, "q1")
                P_chunk(gt, 0, h)
                between()
            together(lambda: [mm(R("PSM", 64 * h, 64 * h + 64), R("SEL2", 128 * i, 128 * i + 128), R("mx", 1024 * h + i, 1024 * h + 1024, 16),
                                 i == 0, i == 15) for i in range(16)])

    def list_table():
        act(R("cR"), IX(R("IW", 0, 4096), R("c16")), scale=2048.0)
        dma("y", T.K[0:128:2, :], T.cR[0:128:16, :], [("cR", 0, 2048)], [("K", 0, 256)])
        dma("y", T.K[1:128:2, :], T.cR[0:128:16, :], [("cR", 0, 2048)], [("K", 256, 512)])

    def tree(src, out, op):
        tt(R("red", 0, 64), R(src, 0, 64), R(src, 64, 128), op)
        tt(R("red", 64, 96), R("red", 0, 32), R("red", 32, 64), op)
        tt(out, R("red", 64, 80), R("red", 80, 96), op)

    def flags_front():
        hash_front()
        tt(R("d1"), R("PSM", 0, 128), R("sm"), OP.subtract)
        tt(R("bd"), R("d1"), Pthr, OP.is_gt)
        tree("bd", L("tr"), OP.add)

    for h in range(2): P_chunk("V", E0, h)
    hash_front()
    cp(PsE, R("sm"))
    gather_front(0, lambda: None)
    hash_back("yI1")
    cp(R("NCE"), R("yI1"))
    ts(Pthr, PsE, 150.0, OP.add)
    ts(R("t2"), R("t1"), -1.0 / 32, OP.mult, 1.0 / 32, OP.add)
    tree("t2", L("n32"), OP.add)
    flags_front()
    tt(R("code0"), L("tr"), L("n32"), OP.add)
    out_send(0, "co", R("code0"))
    hash_back("yI0")
    out_send(0, "nc", R("yI0"))
    cp(L("cur"), R("jW", 0, 16)); cp(R("cur16"), L("cur"))
    scatter_act(IX(R("LK"), R("ei16")), R("LV0"))
    list_table()
    lna = math.log(1.75)
    ts(L("lm"), R("jW", 0, 16), -128.0, OP.add)
    act(L("wW"), L("lm"), AF.Exp, -lna)
    ts(R("thrR"), R("OR"), -128.0, OP.add)
    act(R("thrR"), R("thrR"), AF.Exp, -lna)
    ts(R("thrR"), R("thrR"), 2.5, OP.mult)
    ts(Pkb, Pk, 4096.0, OP.mult)
    ts(R("t1"), R("t1"), 65536.0, OP.mult)
    tt(R("HB"), R("t1"), Pkb, OP.add)
    ts(R("kp1"), Pk, 1.0, OP.add)
    ts(C(6), C(0), 0.0, OP.is_equal)
    ts(C(7), C(0), 1.0, OP.is_equal)
    ts(C(8), C(0), 1.0, OP.add, 0.5, OP.mult)
    for t in range(STEPS):
        ts(C(10 + t), C(1), float(t + 2), OP.mult, 64.0, OP.add)
    fill(C(16), -2048.0); fill(C(17), -64.0)
    ts(R("PKP"), R("B128"), C(6), OP.mult)
    ts(R("PKH"), R("B128"), C(6), OP.mult)
    ts(R("PKO"), R("B128"), C(7), OP.mult)
    cp(R("B8"), R("B128", 0, 128, 16))
    cp(R("B8H"), R("B128", 0, 128, 16))
    ts(R("MK"), R("clOp"), C(0), OP.is_equal)
    mm(R("PSD", 0, 128, 1, 8), R("PKP", 0, 128, 16), R("PKP"), True, True)
    cp(R("PK8", 0, 128, 1, 8), R("PSD", 0, 128, 1, 8))
    ts(R("JC"), R("OR"), C(3), OP.add)
    ts(R("DUM", 0, 24), R("jW", 0, 24), 4096.0, OP.add, 2048.0, OP.mult)
    ts(R("DUM", 24, 48), R("jW", 0, 24), 4096.0, OP.add, 2048.0, OP.mult)
    ts(L("dm256"), R("jW", 0, 16), 256.0, OP.add)
    ts(L("dm4096"), R("jW", 0, 16), 4096.0, OP.add)
    fill(L("z"), 0.0); fill(L("dec"), 0.0); fill(R("ZB"), 0.0)
    fill(R("V", DB, E1), 0.0)
    ts(R("BTM"), R("BTM"), -1.0, OP.mult)
    cp(R("dec16"), L("dec"))

    def renew_state(y):
        tt(R("t1"), R("sm"), PsE, OP.subtract)
        tt(R("t1"), R("t1"), Pdp, OP.mult)
        tt(PsE, PsE, R("t1"), OP.add)
        tt(R("t2"), R(y), R("NCE"), OP.subtract)
        tt(Pt, R("t2"), Pdp, OP.mult)
        tt(R("NCE"), R("NCE"), Pt, OP.add)

    def lanes_pre(t, between):
        tt(R("key"), R("HB"), Pc, OP.add)
        tree("key", L("keyv"), OP.min)
        cp(R("keI"), L("keyv"))
        ts(R("ceI"), R("keI"), 4095, OP.bitwise_and)
        ts(L("full"), L("keyv"), 65536.0, OP.is_ge, 4096.0, OP.mult)
        tt(L("x1"), R("ceI"), L("full"), OP.max)
        cp(R("cl16"), L("x1"))
        act(R("clOp"), IX(R("IW"), R("cl16")))
        act(R("clR"), IX(R("clOp"), R("cur16")), bias=C(16))
        act(R("decR"), IX(R("IW", 0, 8), R("dec16")), scale=-1.0)
        act(R("OPW", 0, 256), R("ZB"))
        act(R("LV"), IX(R("IW", 0, 256), R("cur16")), scale=C(2), bias=C(10 + t))
        conv1("PSA", [("clR", 128, R("PKH"))])
        ts(R("fkI"), R("keI"), 12, OP.arith_shift_right)
        ts(L("fk1"), R("fkI"), 1.0, OP.add)
        ts(R("acI"), R("wkI"), t, OP.arith_shift_right, 1, OP.bitwise_and)
        cp(L("act"), R("acI"))
        act(R("COMP", 0, 48), R("DUM"))
        between()
        conv2("PSA", 0, "qh", "B8H")
        tt(R("t4"), Pkb, R("HB"), OP.subtract)
        cp(L("clS"), R("PSA", 0, 16))
        ts(L("cl"), L("clS"), 2048.0, OP.add)
        cp(R("lc16"), L("cl"))
        act(R("G1"), IX(R("LK", 0, LW), R("lc16")), bias=C(17))

    def judge(t):
        tt(L("X"), R("code%d" % (t & 1)), R("lc%d" % t), OP.add)
        ts(R("rdy"), L("X"), 0.0, OP.is_equal)
        together(lambda: [mm(R("PSR", 0, 16), R("B128"), R("rdy"), True, True), mm(R("PSR", 16, 32), R("BTM"), R("rdy"), True, True)])
        conv1("PSA", [("G1", 128, R("PKP"))])
        ts(R("cab", 16, 32), L("X"), 1.0, OP.is_ge)
        ts(L("nr"), L("X"), 0.0, OP.is_gt)
        tt(L("e"), L("dm256"), L("nr"), OP.mult)
        comp("v", [R("PSR", 0, 16), L("z")], [L("inc")],
             lambda r, w: g.vector.tensor_tensor_scan(ap(w[0]), ap(r[0]), ap(r[1]), 0.0, OP.add, OP.add))
        tt(L("rank"), R("PSR", 16, 32), L("inc"), OP.add)
        ts(L("cm"), L("rank"), 48.0, OP.is_lt)
        tt(R("cab", 0, 16), L("cm"), R("rdy"), OP.mult)
        tt(L("done"), R("cab", 0, 16), R("cab", 16, 32), OP.add)
        cp(R("dn16"), L("done"))
        act(R("dnR"), IX(R("IW", 0, 8), R("dn16")))
        act(R("gnR"), IX(R("dnR"), R("cur16")))
        tt(L("x5"), L("rank"), L("e"), OP.max)
        cp(R("off16"), L("x5"))
        conv2("PSA", 16, "q0")
        together(lambda: [mm(R("PSC", 128 * j + 16 * k, 128 * j + 16 * k + 16), R("ID"), R("cab", 16 * j, 16 * j + 16), True, True)
                          for j in range(2) for k in range(8)])
        conv1("PSR", [("gnR", 128, R("PKP"))])
        comp("v", [("n", "K", 0, 512, 1, 128), R("JC")], [IX(R("COMP"), R("off16"))],
             lambda r, w: g.vector.tensor_tensor(out=ap(w[0]), in0=T.K[:], in1=T.JC[:], op=OP.add))
        cp(R("p16"), R("PSA", 16, 32))
        cp(L("p"), R("p16"))
        ts(R("Lt", 0, 24), R("COMP", 0, 24), C(2), OP.mult)
        ts(R("Lt", 24, 48), R("COMP", 24, 48), C(1), OP.mult)
        tt(R("Ls", 0, 24), R("Lt", 0, 24), R("Lt", 24, 48), OP.add)
        ts(R("Ls", 24, 48), R("Ls", 0, 24), 2047, OP.bitwise_and)
        cp(R("L16", 0, 24), R("Ls", 24, 48))
        act(R("decL"), IX(R("decR"), R("p16")))
        act(R("Dl"), IX(R("lb%d" % t), R("L16", 0, 24)))
        conv1("PSA", [("G1", 128, R("PKO")), ("decL", 128, R("PKP"))])
        ts(R("Ls", 48, 72), R("Ls", 0, 24), 11, OP.arith_shift_right)
        cp(R("L16", 24, 48), R("Ls", 48, 72))
        conv2("PSR", 32, "q1")
        for c in range(16):
            ts(R("EQ", 272 * c, 256 * c + 256), R("clR", 16 * c, 256), L("clS", c, c + 1), OP.is_equal)
        conv2("PSA", 32, "q0")
        ts(L("nf"), L("cl"), 4096.0, OP.is_lt)
        tt(L("an"), L("act"), L("nf"), OP.mult)
        tt(R("t3"), R("NCE"), Pc, OP.subtract)
        ts(L("val"), R("PSA", 32, 48), 0.0, OP.is_gt)
        tt(L("mv"), L("an"), L("val"), OP.mult)
        tt(L("cand"), L("an"), L("mv"), OP.subtract)

    def lanes_moves():
        tt(L("x1"), L("p"), L("cur"), OP.subtract)
        tt(L("x1"), L("x1"), L("mv"), OP.mult)
        tt(L("cur1"), L("cur"), L("x1"), OP.add)
        tt(L("x4"), R("jW", 0, 16), L("cur1"), OP.subtract)
        tt(L("x4"), L("x4"), R("PSR", 32, 48), OP.mult)

    def new_cells(t):
        tt(R("t1"), R("ln%d" % t), Pc, OP.subtract)
        tt(R("t1"), R("t1"), R("PSC", 0, 128), OP.mult)
        tt(R("t2"), R("t3"), R("PSC", 128, 256), OP.mult)
        tt(Pc, Pc, R("t1"), OP.add)
        tt(Pc, Pc, R("t2"), OP.add)
        cp(R("c16"), Pc)

    def commit_columns():
        cp(IX(R("V", VB, E1), R("L16", 24, 48)), R("Dl"))

    def masks():
        cp(R("cmS"), R("PSC", 0, 128))
        tt(Pdp, R("PSC", 128, 256), R("cmS"), OP.add)

    def thresholds():
        ts(R("t1"), Pdp, BIG, OP.mult, 150.0, OP.add)
        tt(Pthr, PsE, R("t1"), OP.add)

    def lanes_claim():
        ts(L("x6"), R("PSR", 32, 48), -1.0, OP.mult, 1.0, OP.add)
        tt(L("ac"), L("x6"), L("cand"), OP.mult)
        tt(L("aw"), L("ac"), L("wW"), OP.mult)
        for k in range(8):
            ts(R("LH", 16 * k, 16 * k + 16), L("aw"), R("GC", k, k + 1), OP.mult)
        together(lambda: [mm(R("PSA", 16 * c, 256, 1, 8), R("LH", c, 128, 16), R("EQ", 272 * c, 256 * c + 256), c == 0, c == 15) for c in range(16)])

    def lanes_out(t):
        tt(L("win"), L("ac"), R("PSD", 0, 16), OP.mult)
        ts(L("lose"), L("win"), -1.0, OP.mult, 1.0, OP.add)
        tt(L("x1"), L("lose"), L("dm256"), OP.mult)
        tt(L("x1"), L("x1"), L("cur"), OP.max)
        cp(R("oo16"), L("x1"))
        cp(IX(R("OPW"), R("oo16")), R("ONE"))
        conv1("PSD", [("OPW", 128, R("PKP"))])
        lanes_moves()
        conv2("PSD", 16, "q1")
        if t < STEPS - 1:
            tt(L("x5"), L("lose"), L("dm4096"), OP.mult)
            tt(L("x5"), L("x5"), L("cl"), OP.max)
            cp(R("ol16"), L("x5"))
            ts(L("x6"), L("n32"), -1.0, OP.mult, 0.25, OP.add)
            tt(L("x6"), L("x6"), L("done"), OP.mult)
            tt(L("n32a"), L("n32"), L("x6"), OP.add)
            ts(L("x6"), L("done"), float(t + 2), OP.mult)
            tt(L("dec"), L("dec"), L("x6"), OP.max)
            cp(R("dec16"), L("dec"))
            tt(L("cur"), L("cur1"), L("x4"), OP.add)
            cp(R("cur16"), L("cur"))
        else:
            tt(L("cur"), L("cur1"), L("x4"), OP.add)

    def holders():
        tt(R("rw"), L("fk1"), R("PSD", 16, 32), OP.mult)
        together(lambda: [mm(R("PSD", 128 + 16 * k, 144 + 16 * k), R("ID"), R("rw"), True, True) for k in range(8)])

    def holders2():
        tt(Pt, R("t4"), Pdp, OP.mult)
        tt(R("HB"), R("HB"), Pt, OP.add)
        tt(R("t5"), R("PSD", 128, 256), R("kp1"), OP.is_equal)
        ts(Pu, R("t5"), 65536.0, OP.mult)
        tt(R("HB"), R("HB"), Pu, OP.add)

    def snap_window():
        if Ecur[0] == E0: return E0, E1, E1, "eaA", "ejA"
        return VB, VE, E0, "eaB", "ejB"

    def snap_index():
        lo, hi, new, ea, ej = snap_window()
        tt(R("t5"), R(ea), Pc, OP.add)
        tt(Pt, R("t5"), Pdp, OP.mult)
        tt(R("t5"), R(ej), Pt, OP.add)
        cp(R("ei16"), R("t5"))

    def snap_gather():
        lo, hi, new, ea, ej = snap_window()
        act(R("V", new, new + 2048), IX(R("V", lo, hi), R("ei16")))
        Ecur[0] = new

    def const_last():
        cp(R("GC"), R("B128", 0, 128, 16))
        for ea, ej, vb, eb in (("eaA", "ejA", VB - E0, 0), ("eaB", "ejB", 0, E1 - VB)):
            ts(R(ej), R("jW"), float(eb), OP.add)
            ts(R(ea), R("jW"), -1.0, OP.mult, float(vb - eb), OP.add)

    lanes_pre(0, const_last)
    for t in range(STEPS):
        judge(t)
        lanes_claim()
        new_cells(t)
        commit_columns()
        if t == STEPS - 1: break
        n = t + 1
        gather_front(n, lambda: lanes_out(t))
        list_table()
        masks()
        thresholds()
        if t < STEPS - 2:
            snap_index()
            snap_gather()
        if t == 0: act(R("SELW"), R("SEL2"), scale=C(8))
        scatter_act(IX(R("LK", 0, 4352), R("ol16")), R("LV"))
        flags_front()
        ts(L("wo"), R("PSD", 16, 32), -1.0 / 32, OP.mult)
        tt(L("n32"), L("n32a"), L("wo"), OP.add)
        tt(R("code%d" % (n & 1)), L("tr"), L("n32"), OP.add)
        out_send(n, "co", R("code%d" % (n & 1)))
        holders()
        hash_back("yI%d" % (n & 1))
        out_send(n, "nc", R("yI%d" % (n & 1)))
        holders2()
        lanes_pre(n, lambda: renew_state("yI%d" % (n & 1)))
    t = STEPS - 1
    masks()

    def weigh(a, b2):
        for b in range(a, b2):
            mm(R("PSP", 0, 256), R("SELW", 128 * b, 128 * b + 128), R("V", VB + 256 * b, VB + 256 * b + 256), b == 0, b == 15)

    weigh(0, 3)
    lanes_win()
    conv2("PSD", 0, "q1")
    cp(R("sm"), Pc)
    dma("y", T.yc[:], T.sm[:], [("sm", 0, 128)], [])
    weigh(3, 10)
    lanes_out(t)
    last = res(L("cur"))
    dma("s", T.yl[:], ap(last), flat(last), [])
    holders()
    weigh(10, 16)
    holders2()
    ts(R("d1"), R("HB"), 65536.0, OP.is_ge)
    dma("y", T.yh[:], T.d1[:], [("d1", 0, 128)], [])
    cp(R("yso"), R("PSP", 0, 256))
    dma("s", T.ys[:], T.yso[:], [("yso", 0, 256)], [])
    build()
    for sem in sorted(cnt):
        if known["g"].get(sem, 0) < cnt[sem]:
            g.wait_ge(T.sem[sem], cnt[sem])
